import numpy as np, ml_dtypes
CORES = [2,6,10,14,18,22,26,30]
N = 8
BF = ml_dtypes.bfloat16
def gentries(a):
    return np.ascontiguousarray(a.reshape(8, 16, -1).transpose(0, 2, 1)).reshape(8, -1)
def gtable(e):
    e = np.asarray(e); return np.ascontiguousarray(e.reshape(8, -1, 16).transpose(0, 2, 1)).reshape(128, -1).astype(np.int32)
V, S, A, B, T = 2048, 128, 4096, 2, 4
W = V + (N - 1) * S
def parts(rng):
    z = np.exp2(rng.integers(-1, 2, (N, 8, 16, 1))).astype(np.float32); x = {}
    x["h"] = rng.standard_normal((N, 8, 16, V), dtype=np.float32) * z
    x["y"] = rng.standard_normal((N, 8, 16, T), dtype=np.float32) * z
    x["t"] = (z * (0.5 + rng.random(z.shape))).astype(np.float32)
    x["w"] = np.clip(rng.standard_normal((N, 8, 16, A), dtype=np.float32), -2, 2)
    x["M"] = int(rng.integers(0, 60000)) + rng.integers(0, 8, (N, 8, V)); x["m"] = rng.integers(0, A, (N, 8, V))
    x["pd"] = rng.integers(0, W, (N, 8, B, V)); x["lb"] = rng.integers(0, A, (N, 8, B, V)); x["sn"] = rng.integers(0, V, (N, 8, N - 1, S))
    return x
def pack(x):
    def c(a, n):
        v = np.ascontiguousarray(np.reshape(a, (N, 128, n))).astype(np.float32)
        return np.where(np.abs(v) < 2.0 ** -20, np.float32(0), v).astype(np.float32)
    return {"h0": c(x["h"], V), "mt": np.ascontiguousarray(x["M"]).astype(np.int32), "mm": np.ascontiguousarray(x["m"]).astype(np.int32), "wv": c(x["w"], A).astype(BF), "obs": c(x["y"], T), "th": c(x["t"], 1),
            "pd": np.stack([gtable(a.reshape(8, -1)) for a in x["pd"]]), "lb": np.stack([gtable(a.reshape(8, -1)) for a in x["lb"]]), "sn": np.stack([gtable(a.reshape(8, -1)) for a in x["sn"]])}
def at_ends(rng, lo, hi, v, share):
    return np.where(rng.random(v.shape) < share, np.where(rng.random(v.shape) < 0.5, lo, hi), v)
def setup_inputs(rng):
    return pack(parts(rng))
def setup_inputs_spread(rng):
    x = parts(rng)
    x["h"] = rng.standard_normal((N, 8, 16, V), dtype=np.float32) * np.exp2(rng.integers(-3, 3, (N, 8, 1, V))) * (rng.random((N, 8, 1, V)) > 0.0625)
    x["w"] = x["w"] * np.exp2(rng.integers(-4, 1, (N, 8, 1, A))) * (rng.random((N, 8, 1, A)) > 0.0625)
    top = 4096 * int(rng.integers(1, 15)); kind = np.arange(V) & 3
    x["M"] = np.where(kind == 0, top - 1, np.where(kind == 1, top, top - 12 + np.exp2(5 * rng.random((N, 8, V))).astype(np.int64)))
    s, p = x["sn"], x["pd"]; turn = (rng.integers(0, 2, (N, 8, 1, V)) + np.arange(B)[:, None]) & 1
    x["sn"] = s - (s & 3) + (np.arange(S) & 3)
    x["pd"] = np.where(kind == 3, p, p - (p & 3) + np.where(kind == 2, turn, kind))
    return pack(x)
def setup_inputs_ends(rng):
    x = parts(rng)
    x["M"] = 65535 * rng.integers(0, 2, (N, 8, V)); x["M"][:, 5:] = 65535; x["M"][:, 0] = 0
    x["m"] = (A - 1) * rng.integers(0, 2, (N, 8, V)); x["lb"] = at_ends(rng, 0, A - 1, x["lb"], 0.75)
    x["sn"] = at_ends(rng, 0, V - 1, x["sn"], 0.75); x["pd"] = at_ends(rng, 0, W - 1, x["pd"], 0.75)
    x["pd"][:, 7] = at_ends(rng, 0, V - 1, rng.integers(0, V, (N, B, V)), 0.75)
    x["w"] = at_ends(rng, -2, 2, x["w"], 0.7)
    x["t"][:, 0, :15] = 1024; x["t"][:, 7, :15] = 0
    for g in (0, 7):
        x["w"][:, g, 15] = rng.choice(np.array([0, 0, -2, 2]), (N, A)); x["h"][:, g, 15] = rng.choice(np.array([0, 1, -1]), (N, V))
        x["y"][:, g, 15] = 0; x["t"][:, g, 15] = 0
    few = [0, 1, V - 1]
    for g in (0, 7):
        x["pd"][:, g][..., few] = V - 1; x["m"][:, g][..., few] = A - 1
    x["lb"][:, 7][..., few] = A - 1; x["h"][:, 7, 15][..., few] = 1; x["h"][:, 0, 15][..., few] = 0
    a = A - 1
    for _ in range(T):
        a = (4 * a + A - 1) & (A - 1); x["w"][:, 7, 15, a] = 2
    return pack(x)
def setup_inputs_corners(rng):
    x = parts(rng)
    x["sn"][0::2, 1::2] = rng.choice(np.array([0, V - 1]), x["sn"][0::2, 1::2].shape); x["sn"][1::2, 0::2, N - 2] = V - 1
    for q in range(N):
        for g in range(8):
            p, l, kind = x["pd"][q, g], x["lb"][q, g], (g + q) & 7
            if kind == 0: p[:] = np.arange(V); x["M"][q, g] = 65535; x["m"][q, g] = A - 1
            if kind == 1: p[:] = 0; x["M"][q, g] = 0; x["m"][q, g] = 0
            if kind == 2: p[:] = W - 1
            if kind == 3: p[:] = V; p[B - 1, V - 1] = V - 1; x["M"][q, g, V - 1] = 0
            if kind == 4: p[1:] = p[0]; l[1:] = l[0]
            if kind == 5: p[1:] = p[0]; x["m"][q, g] = (A - 1) * rng.integers(0, 2, V)
            if kind == 6: x["t"][q, g] = 1024; x["M"][q, g] = 7
            if kind == 7: x["t"][q, g] = -1024 * (np.arange(16)[:, None] & 1); x["M"][q, g] = 65534 + rng.integers(0, 2, V); x["w"][q, g] = at_ends(rng, -2, 2, x["w"][q, g], 0.5)
    return pack(x)
def setup_inputs_calm(rng):
    x = parts(rng); u = (np.arange(8)[None, :] + np.arange(N)[:, None]) & 3
    x["M"] = u[:, :, None] + rng.integers(0, 2, (N, 8, V))
    n = (rng.random((N, 8, 1, A)) * (2 + u[:, :, None, None])).astype(np.int64)
    x["w"] = np.where(rng.random((N, 8, 16, A)) < 0.0625 * n, x["w"] * 2.0 ** -7, 2.0 ** -20 * rng.integers(-1, 2, (N, 8, 16, A)))
    x["h"] = x["h"] * np.float32(2.0 ** -10); x["t"] = (1 + rng.random((N, 8, 16, 1))).astype(np.float32)
    x["y"] = x["t"] * rng.choice(np.array([-1, 1]), (N, 8, 16, T))
    return pack(x)
def check_inputs(d):
    bad = []
    for k, lo, hi in (("mt", 0, 65535), ("mm", 0, A - 1), ("pd", 0, W - 1), ("lb", 0, A - 1), ("sn", 0, V - 1)):
        if np.min(d[k]) < lo or np.max(d[k]) > hi: bad.append("range of " + k)
    for k, hi in (("wv", 2), ("h0", 65536), ("obs", 65536), ("th", 65536)):
        v = np.abs(d[k].astype(np.float32))
        if not np.max(v) <= hi: bad.append("range of " + k)
        if not np.all((v == 0) | (v >= 2.0 ** -20)): bad.append("least size of " + k)
    return bad
def reference(h0, mt, mm, wv, obs, th, pd, lb, sn):
    h = h0.astype(np.float32).reshape(N, 8, 16, V); M = mt.astype(np.int64); m = mm.astype(np.int64)
    w = wv.astype(np.float32).reshape(N, 8, 16, A); y = obs.astype(np.float32).reshape(N, 8, 16, T); lim = th.astype(np.float32).reshape(N, 8, 16, 1)
    pl = np.stack([gentries(a) for a in pd]).astype(np.int64); ll = np.stack([gentries(a) for a in lb]).astype(np.int64)
    sl = np.stack([gentries(a) for a in sn]).astype(np.int64).reshape(N, 8, N - 1, S)
    for t in range(T):
        hw, Mw, mw = [h], [M], [m]
        for d in range(1, N):
            ix = sl[:, :, d - 1]
            hw.append(np.roll(np.take_along_axis(h, ix[:, :, None, :], 3), (d, -1), (0, 1)))
            Mw.append(np.roll(np.take_along_axis(M, ix, 2), (d, -1), (0, 1))); mw.append(np.roll(np.take_along_axis(m, ix, 2), (d, -1), (0, 1)))
        hp = np.take_along_axis(np.concatenate(hw, axis=3), pl[:, :, None, :], 3)
        Mp = np.take_along_axis(np.concatenate(Mw, axis=2), pl, 2); mp = np.take_along_axis(np.concatenate(mw, axis=2), pl, 2)
        a = (4 * mp + ll) & (A - 1)
        wa = np.take_along_axis(w, a[:, :, None, :], 3)
        e = y[..., t:t + 1] - hp * wa
        c = np.add.reduce((np.abs(e) > lim).astype(np.int64), axis=2)
        new = (Mp + c).reshape(N, 8, B, V); k = np.argmin(new, axis=2)
        pick = k * V + np.arange(V)
        M = np.min(new, axis=2); m = np.take_along_axis(a, pick, 2); p4 = pick[:, :, None, :]
        u = np.take_along_axis(e, p4, 3) * np.take_along_axis(wa, p4, 3)
        h = np.take_along_axis(hp, p4, 3) + np.float32(0.125) * u
    return {"yh": h.reshape(N, 128, V).astype(np.float32), "ymt": M.astype(np.float32), "ymm": m.astype(np.float32)}

@@ -1,0 +1,495 @@
+from concourse.bass import DstId, RemoteDMATransfer
+from concourse.mybir import AluOpType, ActivationFunctionType
+
+V, S, A, NS, N = 2048, 128, 4096, 4, 8
+W = V + (N - 1) * S
+SH = (N - 1) * S
+ASSIST = (3,)
+VIA_M, VIA_H, PE_ROT = (0, 1, 2, 3), (0, 1, 2, 3), True
+ORDER = "v0 w0 v1 w1 i0 i1 x0 v2 w2 y0 i2 v3 w3 i3 p0 a0 x1 p1 a1 y1 p2 a2 p3 a3 c0 c1 c2 c3 d0 e0 e1 d1"
+
+SCRATCH = {
+    "rot": ("sbuf", [128, 128], "float32"),
+    "hw0": ("sbuf", [128, W], "float32"), "hw1": ("sbuf", [128, W], "float32"),
+    "wm0": ("sbuf", [128, W], "bfloat16"), "wm1": ("sbuf", [128, W], "bfloat16"),
+    "wrot": ("sbuf", [128, V], "bfloat16"),
+    "tw": ("sbuf", [128, 2 * A], "bfloat16"),
+    "mp": ("sbuf", [128, 4096], "bfloat16"),
+    "wa": ("sbuf", [128, 4096], "float32"),
+    "pp": ("sbuf", [128, 4096], "float32"),
+    "ab": ("sbuf", [128, 4096], "float32"),
+    "df": ("sbuf", [128, 4096], "bfloat16"),
+    "cm": ("sbuf", [128, 4096], "bfloat16"),
+    "ee": ("sbuf", [128, V], "float32"), "uu": ("sbuf", [128, V], "float32"),
+    "sh": ("sbuf", [128, SH], "float32"), "shr": ("sbuf", [128, SH], "float32"),
+    "sm": ("sbuf", [128, SH], "bfloat16"),
+    "li": ("sbuf", [128, 368], "int32"),
+    "nat": ("sbuf", [128, 368], "uint16"), "per": ("sbuf", [128, 312], "uint16"),
+    "lbi": ("sbuf", [128, 256], "int32"), "lbf": ("sbuf", [128, 256], "float32"),
+    "lbh": ("sbuf", [128, 256], "bfloat16"), "lbl": ("sbuf", [128, 256], "bfloat16"),
+    "mi": ("sbuf", [128, 256], "int32"),
+    "ti": ("sbuf", [128, 256], "int32"), "xi": ("sbuf", [128, 256], "int32"),
+    "dx": ("sbuf", [128, 128], "float32"), "dpd": ("sbuf", [128, 128], "float32"),
+    "kk": ("sbuf", [128, 256], "float32"), "qq": ("sbuf", [128, 256], "float32"),
+    "xx": ("sbuf", [128, 512], "bfloat16"), "n1": ("sbuf", [128, 128], "float32"),
+    "al": ("sbuf", [128, 256], "uint16"), "lst": ("sbuf", [128, 256], "uint16"),
+    "ob": ("sbuf", [128, 4], "float32"), "y8": ("sbuf", [128, 4], "float32"),
+    "tc": ("sbuf", [128, 4], "float32"), "nt": ("sbuf", [128, 4], "float32"),
+    "pi": ("sbuf", [128, 8], "int32"), "pc": ("sbuf", [128, 8], "float32"),
+    "jr": ("sbuf", [128, 144], "float32"), "vi": ("sbuf", [128, 64], "float32"),
+    "ec": ("sbuf", [128, 144], "bfloat16"), "ex": ("sbuf", [128, 144], "bfloat16"), "em": ("sbuf", [128, 144], "bfloat16"),
+    "idn": ("sbuf", [128, 128], "bfloat16"),
+    "t1": ("sbuf", [128, 312], "int32"), "t2": ("sbuf", [128, 312], "int32"),
+    "f1": ("sbuf", [128, 312], "float32"), "f2": ("sbuf", [128, 312], "float32"), "f3": ("sbuf", [128, 312], "float32"),
+    "pt0": ("psum", [128, 512], "float32"), "pt1": ("psum", [128, 512], "float32"),
+    "pt2": ("psum", [128, 512], "float32"), "pt3": ("psum", [128, 512], "float32"),
+    "pn0": ("psum", [128, 512], "float32"), "pn1": ("psum", [128, 512], "float32"),
+    "ps": ("psum", [128, 512], "float32"),
+}
+NDMA = 40
+SEMAPHORES = (["cv", "ca", "ct", "cg"] + ["d%d" % i for i in range(NDMA)] + ["gd0"]
+              + ["am%d" % t for t in range(NS)] + ["ah%d" % t for t in range(NS)]
+              + ["lm%d" % t for t in range(NS)] + ["lh%d" % t for t in range(NS)])
+COUNTER = {"v": "cv", "a": "ca", "t": "ct", "g": "cg"}
+
+
+def routes(core, cores, topo):
+    r = cores.index(core)
+    kinds = {"near": [], "mate": [], "plane": [], "two": []}
+    for d in range(1, N):
+        c = cores[(r + d) % N]
+        a, b = topo.chip(core), topo.chip(c)
+        kinds["near" if a == b else "mate" if topo.mates(a, b) else "plane" if topo.same_plane(a, b) else "two"].append((d, c))
+    free = [h for h in topo.cores_of(core) if h not in cores and topo.die(h) == topo.die(core)]
+    hm = [h for h in free if topo.may_write(h, kinds["mate"][0][1])][0]
+    hs = [h for h in free if h != hm and topo.may_write(h, kinds["plane"][0][1])][0]
+    return kinds, {"mate": hm, "plane": hs}
+
+
+def share(src, dests, topo):
+    es = topo.engines(src, dests[0][1])
+    k = len(es) // len(dests)
+    return [(d, 1, c, es[j * k:(j + 1) * k]) for j, (d, c) in enumerate(dests)]
+
+
+def calls_of(core, cores, topo, via):
+    if core not in cores:
+        for q in cores:
+            kinds, hand = routes(q, cores, topo)
+            for k in hand:
+                if via and hand[k] == core:
+                    return [share(core, kinds[k], topo)]
+        return []
+    kinds, hand = routes(core, cores, topo)
+    off = topo.engines(core, kinds["two"][0][1])
+    near = [(d, 1, c, [e for e in topo.engines(core, c) if e not in off]) for d, c in kinds["near"]]
+    if not via:
+        return [share(core, kinds["two"] + kinds["plane"], topo), share(core, kinds["mate"], topo) + near]
+    es = topo.engines(core, hand["mate"])
+    k = len(es) // 2
+    first = [(kinds[n][0][0], 2, hand[n], es[j * k:(j + 1) * k]) for j, n in enumerate(("plane", "mate"))]
+    return [first, share(core, kinds["two"], topo) + near]
+
+
+def arrivals(core, cores, topo, via):
+    senders = set(h for q in cores for h in topo.cores_of(q))
+    return sum(len(e) for q in senders for cl in calls_of(q, cores, topo, via) for _, _, c, e in cl if c == core)
+
+
+def send(g, T, topo, call, src, dst, asem, lsem):
+    tr = []
+    for d, n, c, es in call:
+        rid, pid, _ = topo.addr(c)
+        tr.append(RemoteDMATransfer(dst_ids=[DstId(rid=rid, pnc=pid)], dma_engine_mask=sum(1 << e for e in es),
+                                    remote_sem=T.sem[asem], src=src(d, n), dst=dst(d, n, c)))
+    g.remote_dma_fused(tr, local_sem=T.sem[lsem])
+    return sum(len(es) for _, _, _, es in call)
+
+
+def kinds_of(t):
+    return (("m", "wm", "cm", t in VIA_M), ("h", "hw", "pp", t in VIA_H))
+
+
+def hand_on(g, core, T, topo):
+    cores = list(T.cores)
+    ends = []
+    for t in range(NS):
+        for name, win, land, via in kinds_of(t):
+            for call in calls_of(core, cores, topo, via):
+                d0 = call[0][0]
+                g.wait_ge(T.sem["a%s%d" % (name, t)], arrivals(core, cores, topo, via))
+                n = send(g, T, topo, call, lambda d, n: T[land][:, (2 * t + d - d0) * S:(2 * t + d - d0 + 1) * S],
+                         lambda d, n, c: T["%s%d" % (win, t % 2)][:, V + (d - 1) * S:V + d * S], "a%s%d" % (name, t), "l%s%d" % (name, t))
+                ends.append(("l%s%d" % (name, t), n))
+    for sem, n in ends:
+        g.wait_ge(T.sem[sem], n)
+
+
+def rank_program(g, core, T, topo):
+    rank = T.rank_of(core)
+    if rank is None:
+        hand_on(g, core, T, topo)
+        return
+    cores = list(T.cores)
+    add, sub, mul = AluOpType.add, AluOpType.subtract, AluOpType.mult
+    band, shr_ = AluOpType.bitwise_and, AluOpType.logical_shift_right
+    F = ActivationFunctionType
+    eng = {"v": g.vector, "a": g.scalar, "t": g.tensor, "s": g.sync, "g": g}
+
+    clock = {q: {} for q in eng}
+    count = {}
+    waited = {}
+    order = []
+    acc = {}
+    nd = [0]
+
+    def need(q, tok):
+        sem, val, clk = tok
+        if clock[q].get(sem, 0) >= val:
+            return
+        eng[q].wait_ge(T.sem[sem], val)
+        waited[sem] = max(waited.get(sem, 0), val)
+        for s_, v_ in clk.items():
+            if clock[q].get(s_, 0) < v_:
+                clock[q][s_] = v_
+        clock[q][sem] = val
+
+    def before(q, rd, wr):
+        toks = []
+        for (lst_, w) in ((rd, False), (wr, True)):
+            for (b, lo, hi) in lst_:
+                bank = SCRATCH[b][0] == "psum"
+                for e in acc.get(b, []):
+                    if bank and e[4] != q:
+                        toks.append(e[2])
+                    elif e[0] < hi and lo < e[1] and (w or e[3]) and not (q == "t" and e[4] == "t"):
+                        toks.append(e[2])
+        best = {}
+        for tk in toks:
+            if tk[0] not in best or best[tk[0]][1] < tk[1]:
+                best[tk[0]] = tk
+        for tk in sorted(best.values(), key=lambda x: -len(x[2])):
+            need(q, tk)
+
+    def after(q, rd, wr, tok):
+        for (b, lo, hi) in wr:
+            acc[b] = [e for e in acc.get(b, []) if not (lo <= e[0] and e[1] <= hi)]
+            acc[b].append([lo, hi, tok, True, q])
+        for (b, lo, hi) in rd:
+            acc.setdefault(b, []).append([lo, hi, tok, False, q])
+
+    def bump(sem, n):
+        count[sem] = count.get(sem, 0) + n
+        if sem not in order:
+            order.append(sem)
+        return count[sem]
+
+    def op(q, rd, wr, *fns):
+        before(q, rd, wr)
+        sem = COUNTER[q]
+        for fn in fns:
+            fn().then_inc(T.sem[sem], 1)
+            val = bump(sem, 1)
+        after(q, rd, wr, (sem, val, dict(clock[q])))
+
+    def dma(parts, rd, wr, sem=None):
+        if sem is None:
+            sem = "d%d" % nd[0]
+            nd[0] += 1
+        clk = {}
+        for q in sorted(set(p[0] for p in parts)):
+            before(q, rd, wr)
+            for s_, v_ in clock[q].items():
+                clk[s_] = max(clk.get(s_, 0), v_)
+        for (q, o, i) in parts:
+            if q == "g":
+                g.dma_start(o, i, allow_slow_non_contiguous=True).then_inc(T.sem[sem], 16)
+            else:
+                eng[q].dma_start(o, i).then_inc(T.sem[sem], 16)
+            val = bump(sem, 16)
+        after("dma", rd, wr, (sem, val, clk))
+
+    def exchange(kind, src, t, make):
+        name, win, land, via = kinds_of(t)[kind]
+        dst, asem, lsem = "%s%d" % (win, t % 2), "a%s%d" % (name, t), "l%s%d" % (name, t)
+        calls = calls_of(core, cores, topo, via)
+        make(runs([[((d - 1) * S, (d - 1 + n) * S) for d, n, _, _ in cl] for cl in calls]))
+        for cl in calls:
+            before("g", [(src, (d - 1) * S, (d - 1 + n) * S) for d, n, _, _ in cl], [])
+            val = bump(lsem, send(g, T, topo, cl, lambda d, n: T[src][:, (d - 1) * S:(d - 1 + n) * S],
+                                  lambda d, n, c_: T[dst][:, V + (d - 1) * S:V + d * S] if c_ in cores else T[land][:, 2 * t * S:(2 * t + 2) * S],
+                                  asem, lsem))
+        after("dma", [(src, 0, SH)], [], (lsem, val, dict(clock["g"])))
+        acc[dst] = [e for e in acc.get(dst, []) if e[0] < V]
+        acc[dst].append([V, W, (asem, bump(asem, arrivals(core, cores, topo, via)), {}), True, "dma"])
+
+    def runs(calls):
+        out = []
+        for cl in calls:
+            cur = []
+            for lo, hi in cl:
+                if cur and cur[-1][1] == lo and hi - cur[-1][0] <= 2 * S:
+                    cur[-1] = (cur[-1][0], hi)
+                else:
+                    cur.append((lo, hi))
+            out += cur
+        return out
+
+    def show_m(q, ml):
+        def make(rs):
+            for lo, hi in rs:
+                gather(q, ("sm", lo, hi), ("wrot", 0, V), (ml, 256 + lo // 16, 256 + hi // 16))
+        return make
+
+    def show_h(hn, qs):
+        def make(rs):
+            if not PE_ROT:
+                gather(qs[0], ("sh", 0, 448), (hn, 0, V), ("nat", 312, 340))
+                gather(qs[1], ("sh", 448, SH), (hn, 0, V), ("nat", 340, 368))
+                dma([("s", T.shr[0:112, :], T.sh[16:128, :]), ("a", T.shr[112:128, :], T.sh[0:16, :])], [("sh", 0, SH)], [("shr", 0, SH)])
+                return
+            for j, (lo, hi) in enumerate(rs):
+                gather(qs[1] if j == 1 else qs[0], ("sh", lo, hi), (hn, 0, V), ("nat", 312 + lo // 16, 312 + hi // 16))
+                pt = ("pt%d" % j, 0, hi - lo)
+                op("t", [("rot", 0, 128), ("sh", lo, hi)], [pt], lambda: g.tensor.matmul(c(*pt), T.rot[:, :], c("sh", lo, hi), True, True))
+            for j, (lo, hi) in enumerate(rs):
+                pt = ("pt%d" % j, 0, hi - lo)
+                op("a", [pt], [("shr", lo, hi)], lambda: g.scalar.activation(c("shr", lo, hi), c(*pt), F.Copy))
+        return make
+
+    def c(b, lo, hi):
+        return T[b][:, lo:hi]
+
+    def ts(q_out, q_in, s1, s2, o0, o1=None, extra=()):
+        if o1 is None:
+            op("v", [q_in] + list(extra), [q_out], lambda: g.vector.tensor_scalar(c(*q_out), c(*q_in), s1, None, o0))
+        else:
+            op("v", [q_in] + list(extra), [q_out], lambda: g.vector.tensor_scalar(c(*q_out), c(*q_in), s1, s2, o0, o1))
+
+    def tt(q_out, a, b, o):
+        op("v", [a, b], [q_out], lambda: g.vector.tensor_tensor(c(*q_out), c(*a), c(*b), o))
+
+    def cp(q_out, q_in):
+        op("v", [q_in], [q_out], lambda: g.vector.tensor_copy(c(*q_out), c(*q_in)))
+
+    def gather(q, out, win, off):
+        if q == "v":
+            op("v", [win, off], [out], lambda: g.vector.tensor_copy(c(*out), c(*win).indirect(c(*off))))
+        else:
+            op("a", [win, off], [out], lambda: g.scalar.activation(c(*out), c(*win).indirect(c(*off)), F.Copy))
+
+    def gtt(out, win, off, b, o):
+        op("v", [win, off, b], [out], lambda: g.vector.tensor_tensor(c(*out), c(*win).indirect(c(*off)), c(*b), o))
+
+    def pieces():
+        cp(("xx", 0, 256), ("qq", 0, 256))
+        tt(("xx", 256, 512), ("qq", 0, 256), ("xx", 0, 256), sub)
+
+    def unlist(wm):
+        x = T.xx
+        dma([("s", T.wrot[r:112:16, 0:V], x[16:128, r * 128:(r + 1) * 128]) for r in range(4)]
+            + [("a", T.wrot[112 + r:113 + r, 0:V], x[0:16, r * 128:(r + 1) * 128]) for r in range(4)],
+            [("xx", 0, 512)], [("wrot", 0, V)])
+        dma([("s", T[wm][r:128:16, 0:V], x[:, r * 128:(r + 1) * 128]) for r in range(4)], [("xx", 0, 512)], [(wm, 0, V)])
+
+    LC = [0, 128, 64, 192]
+
+    dma([("s", c("mi", 0, 128), T.mm[:]), ("a", c("mi", 128, 256), T.mt[:])], [], [("mi", 0, 256)])
+    dma([("s", T.li[0:112, 256:312], T.sn[16:128, :]), ("a", T.li[112:128, 256:312], T.sn[0:16, :]),
+         ("a", c("li", 312, 368), T.sn[:])], [], [("li", 256, 368)])
+    dma([("s", c("hw0", 0, V // 2), T.h0[:, 0:V // 2])], [], [("hw0", 0, V // 2)])
+    dma([("s", c("li", 0, 256), T.pd[:]), ("a", c("lbi", 0, 256), T.lb[:]), ("a", c("ob", 0, 4), T.obs[:])], [],
+        [("li", 0, 256), ("lbi", 0, 256), ("ob", 0, 4)])
+    op("g", [], [("pi", 0, 1)], lambda: g.iota(c("pi", 0, 1), [[0, 1]], 0, 1))
+    op("g", [], [("pi", 3, 4)], lambda: g.iota(c("pi", 3, 4), [[0, 1]], 112, 1))
+    op("g", [], [("jr", 0, 144)], lambda: g.iota(c("jr", 0, 144), [[1, 144]], 0, 0, allow_small_or_imprecise_dtypes=True))
+    op("g", [], [("vi", 0, 64)], lambda: g.iota(c("vi", 0, 64), [[16, 64]], 0, 1, allow_small_or_imprecise_dtypes=True))
+    dma([("g", c("tc", 0, 1), T.th[:])], [], [("tc", 0, 4)], sem="gd0")
+    op("v", [], [("wrot", 0, V)], lambda: g.vector.memset(c("wrot", 0, V), 0.0))
+    op("v", [], [("wm0", 0, V)], lambda: g.vector.memset(c("wm0", 0, V), 0.0))
+    ts(("mi", 0, 128), ("mi", 0, 128), 1023, None, band)
+    cp(("qq", 0, 256), ("mi", 0, 256))
+    pieces()
+    cp(("nat", 256, 368), ("li", 256, 368))
+    unlist("wm0")
+    dma([("s", c("hw0", V // 2, V), T.h0[:, V // 2:V])], [], [("hw0", V // 2, V)])
+    dma([("s", c("tw", 0, V), T.wv[:, 0:V])], [], [("tw", 0, V)])
+    ts(("pi", 3, 4), ("pi", 3, 4), 127, None, band)
+    ts(("pi", 1, 2), ("pi", 0, 1), 112, None, band)
+    ts(("pi", 2, 3), ("pi", 0, 1), 13, None, band)
+    cp(("pc", 6, 7), ("pi", 3, 4))
+    cp(("pc", 0, 3), ("pi", 0, 3))
+    ts(("rot", 0, 128), ("jr", 0, 128), c("pc", 6, 7), None, AluOpType.is_equal, extra=[("pc", 6, 7)])
+    ts(("pc", 3, 4), ("pc", 1, 2), 15.0, None, add)
+    ts(("pc", 4, 5), ("pc", 2, 3), 0.0, 4.0, AluOpType.is_equal, mul)
+    ts(("pc", 5, 6), ("pc", 2, 3), 1.0, None, AluOpType.is_equal)
+    ts(("ec", 0, 144), ("jr", 0, 144), c("pc", 3, 4), None, AluOpType.is_equal, extra=[("pc", 3, 4)])
+    ts(("idn", 0, 128), ("jr", 0, 128), c("pc", 0, 1), None, AluOpType.is_equal, extra=[("pc", 0, 1)])
+    exchange(0, "sm", 0, show_m("v", "nat"))
+    exchange(1, "shr", 0, show_h("hw0", "aa"))
+    dma([("a", c("tw", V, A), T.wv[:, V:A])], [], [("tw", V, A)])
+    ts(("ex", 0, 144), ("ec", 0, 144), c("pc", 4, 5), None, mul, extra=[("pc", 4, 5)])
+    ts(("em", 0, 144), ("ec", 0, 144), c("pc", 5, 6), None, mul, extra=[("pc", 5, 6)])
+    cp(("nat", 0, 256), ("li", 0, 256))
+    cp(("lbf", 0, 256), ("lbi", 0, 256))
+    ts(("y8", 0, 4), ("ob", 0, 4), 0.125, None, mul)
+    cp(("lbh", 0, 256), ("lbf", 0, 256))
+    ts(("nt", 0, 1), ("tc", 0, 1), -1.0, None, mul)
+    tt(("lbl", 0, 256), ("lbf", 0, 256), ("lbh", 0, 256), sub)
+    for h in range(2):
+        ts(("kk", 128 * h, 128 * h + 64), ("vi", 0, 64), c("pc", 1, 2), 1.0 / 1024, sub, mul, extra=[("pc", 1, 2)])
+        ts(("kk", 128 * h + 64, 128 * h + 128), ("li", 64 * h, 64 * h + 64), 1.0 / 1024, None, mul)
+    tt(("f1", 0, 128), ("li", 128, 256), ("li", 0, 128), sub)
+    op("v", [], [("wm1", 0, V)], lambda: g.vector.memset(c("wm1", 0, V), 0.0))
+    ts(("dpd", 0, 128), ("f1", 0, 128), 1.0 / 1024, None, mul)
+    ts(("t1", 0, 312), ("li", 0, 312), 15, None, band)
+    ts(("t2", 0, 312), ("li", 0, 312), 4, None, shr_)
+    ts(("f1", 0, 312), ("t1", 0, 312), 128.0, None, mul)
+    ts(("f3", 0, 312), ("li", 0, 312), float(V), None, AluOpType.is_ge)
+    tt(("f1", 0, 312), ("f1", 0, 312), ("t2", 0, 312), add)
+    tt(("f2", 0, 312), ("li", 0, 312), ("f1", 0, 312), sub)
+    tt(("f2", 0, 312), ("f2", 0, 312), ("f3", 0, 312), mul)
+    tt(("f1", 0, 312), ("f1", 0, 312), ("f2", 0, 312), add)
+    cp(("tw", A, A + V), ("tw", 0, V))
+    cp(("per", 0, 312), ("f1", 0, 312))
+    cp(("tw", A + V, 2 * A), ("tw", V, A))
+
+    def listmm(out, lo, n, wt, src, slo, start, stop, pre=()):
+        fns = list(pre)
+        for i in range(16):
+            fns.append(lambda i=i: g.tensor.matmul(T[out][:, lo:lo + n], T[wt][:, 15 - i:143 - i],
+                                                   T[src][:, slo + i:slo + 16 * n:16], start and i == 0, stop and i == 15))
+        rd = [(wt, 0, 144), (src, slo, slo + 16 * n)]
+        if pre:
+            rd += [("idn", 0, 128), ("lbh", 0, 256), ("lbl", 0, 256)]
+        op("t", rd, [(out, lo, lo + n)], *fns)
+
+    for t in range(NS):
+        last = t == NS - 1
+        hw, hn = "hw%d" % (t % 2), "hw%d" % ((t + 1) % 2)
+        wm, wn = "wm%d" % (t % 2), "wm%d" % ((t + 1) % 2)
+        ml = "nat" if t == 0 else "per"
+
+        def gm(q, k):
+            gather(q, ("mp", 1024 * k, 1024 * k + 1024), (wm, 0, W), (ml, LC[k], LC[k] + 64))
+            pt = "pt%d" % k
+            listmm(pt, 0, 64, "ex", "mp", 1024 * k, False, True, pre=[
+                lambda: g.tensor.matmul(c(pt, 0, 64), T.idn[:, :], c("lbh", LC[k], LC[k] + 64), True, False),
+                lambda: g.tensor.matmul(c(pt, 0, 64), T.idn[:, :], c("lbl", LC[k], LC[k] + 64), False, False)])
+
+        def cvt(k):
+            cp(("al", 64 * k, 64 * k + 64), ("pt%d" % k, 0, 64))
+
+        def gw(q, k):
+            gather(q, ("wa", 1024 * k, 1024 * k + 1024), ("tw", 0, 2 * A), ("al", 64 * k, 64 * k + 64))
+
+        def prod(k):
+            r = (1024 * k, 1024 * k + 1024)
+            gtt(("pp",) + r, (hw, 0, W), ("nat", LC[k], LC[k] + 64), ("wa",) + r, mul)
+
+        def absd(k):
+            r = (1024 * k, 1024 * k + 1024)
+            op("a", [("pp",) + r, ("ob", 0, 4)], [("ab",) + r],
+               lambda: g.scalar.activation(c("ab", *r), c("pp", *r), F.Abs, bias=c("ob", t, t + 1), scale=-1.0))
+            if k in ASSIST:
+                op("a", [("ab",) + r, ("nt", 0, 1)], [("df",) + r],
+                   lambda: g.scalar.activation(c("df", *r), c("ab", *r), F.Identity, bias=c("nt", 0, 1), scale=1.0))
+
+        def comp(k):
+            r = (1024 * k, 1024 * k + 1024)
+            if k in ASSIST:
+                ts(("cm",) + r, ("df",) + r, 0.0, None, AluOpType.is_gt)
+            else:
+                ts(("cm",) + r, ("ab",) + r, c("tc", 0, 1), None, AluOpType.is_gt, extra=[("tc", 0, 1)])
+            listmm("pn%d" % (k // 2), 64 * (k % 2), 64, "ec", "cm", 1024 * k, False, k % 2 == 1)
+
+        def decide(h, with_pieces):
+            pn = "pn%d" % h
+            n1 = ("n1", 64 * h, 64 * h + 64)
+            cp(n1, (pn, 64, 128))
+            tt(("ps", 0, 64), (pn, 0, 64), n1, AluOpType.is_gt)
+            tt(("qq", 128 + 64 * h, 192 + 64 * h), (pn, 0, 64), n1, AluOpType.min)
+            tt(("ps", 128, 192), ("ps", 0, 64), ("dx", 64 * h, 64 * h + 64), mul)
+            tt(("ps", 64, 128), ("ps", 0, 64), ("dpd", 64 * h, 64 * h + 64), mul)
+            tt(("qq", 64 * h, 64 * h + 64), ("ps", 128, 192), ("xi", 128 * h, 128 * h + 64), add)
+            tt(("ps", 256, 384), ("ps", 0, 128), ("kk", 128 * h, 128 * h + 128), add)
+            if with_pieces:
+                cp(("xx", 0, 256), ("qq", 0, 256))
+            ts(("lst", 128 * h, 128 * h + 128), ("ps", 256, 384), 1024.0, None, mul)
+            if with_pieces:
+                tt(("xx", 256, 512), ("qq", 0, 256), ("xx", 0, 256), sub)
+
+        def err(h, lo, n):
+            o = ("ee", 1024 * h + lo, 1024 * h + lo + n)
+            win, off = ("pp", 2048 * h, 2048 * h + 2048), ("lst", 128 * h + lo // 16, 128 * h + (lo + n) // 16)
+            op("a", [win, off, ("y8", 0, 4)], [o],
+               lambda: g.scalar.activation(c(*o), c(*win).indirect(c(*off)), F.Identity, bias=c("y8", t, t + 1), scale=-0.125))
+
+        def upd(h, lo, n):
+            r = (1024 * h + lo, 1024 * h + lo + n)
+            gtt(("uu",) + r, ("wa", 2048 * h, 2048 * h + 2048), ("lst", 128 * h + lo // 16, 128 * h + (lo + n) // 16), ("ee",) + r, mul)
+
+        def new(h, lo, n):
+            r = (1024 * h + lo, 1024 * h + lo + n)
+            gtt((hn,) + r, (hw, 0, W), ("lst", 128 * h + 64 + lo // 16, 128 * h + 64 + (lo + n) // 16), ("uu",) + r, add)
+            if last:
+                dma([("s", T.yh[:, r[0]:r[1]], c(hn, *r))], [(hn,) + r], [])
+
+        gm("a", 0)
+        gm("v", 1)
+        gm("a", 2)
+        gm("v", 3)
+        for h in range(2):
+            listmm("pn%d" % h, 0, 128, "em", "mp", 2048 * h, True, False)
+        for w in ORDER.split():
+            k = int(w[1])
+            if w[0] == "v":
+                cvt(k)
+            elif w[0] == "i":
+                cp(("ti", 64 * k, 64 * k + 64), ("pt%d" % k, 0, 64))
+            elif w[0] == "x":
+                ts(("xi", 128 * k, 128 * k + 128), ("ti", 128 * k, 128 * k + 128), A - 1 if last else 1023, None, band)
+            elif w[0] == "y":
+                tt(("dx", 64 * k, 64 * k + 64), ("xi", 128 * k + 64, 128 * k + 128), ("xi", 128 * k, 128 * k + 64), sub)
+            elif w[0] == "w":
+                gw("a", k)
+            elif w[0] == "W":
+                gw("v", k)
+            elif w[0] == "p":
+                prod(k)
+            elif w[0] == "a":
+                absd(k)
+            elif w[0] == "c":
+                comp(k)
+            elif w[0] == "d":
+                decide(k, k == 1 and not last)
+            elif w[0] == "e":
+                err(0, 512 * k, 512)
+            elif w[0] == "u":
+                upd(0, 512 * k, 512)
+        if not last:
+            unlist(wn)
+        else:
+            dma([("s", T.ab[0:8, 0:V], c("qq", 0, 128)), ("s", T.ab[8:16, 0:V], c("qq", 128, 256))], [("qq", 0, 256)], [("ab", 0, V)])
+        err(1, 0, 1024)
+        for k in range(2):
+            if "u%d" % k not in ORDER:
+                upd(0, 512 * k, 512)
+        new(0, 0, 1024)
+        if not last:
+            exchange(0, "sm", t + 1, show_m("a", "per"))
+            upd(1, 0, 1024)
+            new(1, 0, 1024)
+            exchange(1, "shr", t + 1, show_h(hn, "va"))
+        else:
+            op("a", [("ab", 0, V)], [("ab", V, 2 * V)],
+               *[lambda i=i: g.scalar.activation(T.ab[0:16, V + i:2 * V:16], T.ab[0:16, 128 * i:128 * i + 128], F.Copy) for i in range(16)])
+            dma([("a", T.ymm[:], T.ab[0:8, V:2 * V]), ("a", T.ymt[:], T.ab[8:16, V:2 * V])], [("ab", V, 2 * V)], [])
+            upd(1, 0, 1024)
+            new(1, 0, 512)
+            new(1, 512, 256)
+            new(1, 768, 256)
+
+    for sem in order:
+        if waited.get(sem, 0) < count[sem]:
+            g.wait_ge(T.sem[sem], count[sem])

@@ -4,9 +4,21 @@ from concourse.mybir import AluOpType, ActivationFunctionType
 V, S, A, NS, N = 2048, 128, 4096, 4, 8
 W = V + (N - 1) * S
 SH = (N - 1) * S
-ASSIST = (3,)
-VIA_M, VIA_H, PE_ROT = (0, 1, 2, 3), (0, 1, 2, 3), True
-ORDER = "v0 w0 v1 w1 i0 i1 x0 v2 w2 y0 i2 v3 w3 i3 p0 a0 x1 p1 a1 y1 p2 a2 p3 a3 c0 c1 c2 c3 d0 e0 e1 d1"
+
+HEAD = ("A0v.0 A0a.1 A1a.0 A2a.1 A1v.1 X0 o0 X1 A2v.0 o1 B0a X2 A3v.1 B1v.1 A3a.0 X3 Y3 B1a.0 Y0 o2 C0 B2a o3 D0 Y1 C1 i0 D1 C2 "
+        "Y2 S0.0 E0.1 B3a D2.0 i1 E0.0 Z0 E1 D2.1 Z1 i2 n0 S2.0 N0 M0 x0 C3 E2.0 Q0 s0 p0 q0 E2.1 Z2 c0 r0 D3 t0 "
+        "ea0-1 n1 m0 N1 E3 Z3 Q1 h0a ")
+STEP = HEAD + ("u0-1 ea2-3 l0v s1 t1 p1 M1 r1 u2-3 m1 h1a U0 l1v U1 U2 q1 c1 w0-3 ea6-7 ea4-5 u6-7 u4-5 gMa gPa gNa gTa +m "
+               "w4-7 GMv GPa GNa GTv KMa KPa KTa KNv +h")
+LAST = HEAD + "O0 u0-1 ea2-3 s1 t1 p1 M1 r1 m1 q1 w0-1 h1a O1 c1 ea4-5 u2-3 ea6-7 w2-3 u4-5 w4-5 R1 u6-7 w6-6 w7-7"
+FIRST = "*o *w gMv gPv gTv gNv +m GMa GPa KMa GTa KPa GNa KTa KNa +h *d"
+P3 = [["M:x:all0/1"], ["P0:y:on0/1", "P1:z:off0/1"], ["T0:-:off0/2", "T1:-:off1/2", "N:-:on0/1"]]
+PLAN_M = [P3, P3, P3, P3]
+PLAN_H = [P3, P3, P3, P3]
+WV = 2048
+H0 = 768
+WRAP = "ss"
+TURN = 4
 
 SCRATCH = {
     "rot": ("sbuf", [128, 128], "float32"),
@@ -23,15 +35,23 @@ SCRATCH = {
     "ee": ("sbuf", [128, V], "float32"), "uu": ("sbuf", [128, V], "float32"),
     "sh": ("sbuf", [128, SH], "float32"), "shr": ("sbuf", [128, SH], "float32"),
     "sm": ("sbuf", [128, SH], "bfloat16"),
+    "r1": ("sbuf", [16, 16, 128], "float32"), "r2": ("sbuf", [16, V], "float32"),
     "li": ("sbuf", [128, 368], "int32"),
     "nat": ("sbuf", [128, 368], "uint16"), "per": ("sbuf", [128, 312], "uint16"),
     "lbi": ("sbuf", [128, 256], "int32"), "lbf": ("sbuf", [128, 256], "float32"),
     "lbh": ("sbuf", [128, 256], "bfloat16"), "lbl": ("sbuf", [128, 256], "bfloat16"),
     "mi": ("sbuf", [128, 256], "int32"),
-    "ti": ("sbuf", [128, 256], "int32"), "xi": ("sbuf", [128, 256], "int32"),
-    "dx": ("sbuf", [128, 128], "float32"), "dpd": ("sbuf", [128, 128], "float32"),
+    "ti": ("sbuf", [128, 256], "int32"),
+    "xq": ("sbuf", [128, 8, 64], "float32"),
+    "sg": ("sbuf", [128, 128], "bfloat16"), "rr": ("sbuf", [128, 128], "float32"),
+    "tm": ("sbuf", [128, 128], "float32"), "tp": ("sbuf", [128, 128], "float32"),
+    "hi": ("sbuf", [128, 128], "float32"), "ni": ("sbuf", [128, 128], "float32"), "oi": ("sbuf", [128, 128], "float32"),
+    "nid": ("sbuf", [128, 128], "bfloat16"), "i512": ("sbuf", [128, 128], "bfloat16"),
+    "x2": ("sbuf", [128, 8, 64], "float16"), "tm2": ("sbuf", [128, 128], "float16"),
+    "hi2": ("sbuf", [128, 128], "float16"), "ni2": ("sbuf", [128, 128], "float16"), "oi2": ("sbuf", [128, 128], "float16"),
+    "kh": ("sbuf", [128, 256], "float16"), "kl": ("sbuf", [128, 256], "float16"),
     "kk": ("sbuf", [128, 256], "float32"), "qq": ("sbuf", [128, 256], "float32"),
-    "xx": ("sbuf", [128, 512], "bfloat16"), "n1": ("sbuf", [128, 128], "float32"),
+    "xx": ("sbuf", [128, 4, 128], "bfloat16"),
     "al": ("sbuf", [128, 256], "uint16"), "lst": ("sbuf", [128, 256], "uint16"),
     "ob": ("sbuf", [128, 4], "float32"), "y8": ("sbuf", [128, 4], "float32"),
     "tc": ("sbuf", [128, 4], "float32"), "nt": ("sbuf", [128, 4], "float32"),
@@ -40,84 +60,100 @@ SCRATCH = {
     "ec": ("sbuf", [128, 144], "bfloat16"), "ex": ("sbuf", [128, 144], "bfloat16"), "em": ("sbuf", [128, 144], "bfloat16"),
     "idn": ("sbuf", [128, 128], "bfloat16"),
     "t1": ("sbuf", [128, 312], "int32"), "t2": ("sbuf", [128, 312], "int32"),
-    "f1": ("sbuf", [128, 312], "float32"), "f2": ("sbuf", [128, 312], "float32"), "f3": ("sbuf", [128, 312], "float32"),
-    "pt0": ("psum", [128, 512], "float32"), "pt1": ("psum", [128, 512], "float32"),
-    "pt2": ("psum", [128, 512], "float32"), "pt3": ("psum", [128, 512], "float32"),
+    "f1": ("sbuf", [128, 312], "float32"),
+    "pa0": ("psum", [128, 512], "float32"), "pa1": ("psum", [128, 512], "float32"), "pa2": ("psum", [128, 512], "float32"),
     "pn0": ("psum", [128, 512], "float32"), "pn1": ("psum", [128, 512], "float32"),
+    "pn2": ("psum", [128, 512], "float32"), "pn3": ("psum", [128, 512], "float32"),
     "ps": ("psum", [128, 512], "float32"),
 }
-NDMA = 40
-SEMAPHORES = (["cv", "ca", "ct", "cg"] + ["d%d" % i for i in range(NDMA)] + ["gd0"]
+NDMA = 64
+SEMAPHORES = (["cv", "ca", "ct", "cg"] + ["d%d" % i for i in range(NDMA)] + ["gd0", "gd1", "go"]
               + ["am%d" % t for t in range(NS)] + ["ah%d" % t for t in range(NS)]
               + ["lm%d" % t for t in range(NS)] + ["lh%d" % t for t in range(NS)])
 COUNTER = {"v": "cv", "a": "ca", "t": "ct", "g": "cg"}
 
 
-def routes(core, cores, topo):
+def destinations(core, cores, topo):
     r = cores.index(core)
-    kinds = {"near": [], "mate": [], "plane": [], "two": []}
+    kinds = {"N": [], "M": [], "P": [], "T": []}
     for d in range(1, N):
         c = cores[(r + d) % N]
         a, b = topo.chip(core), topo.chip(c)
-        kinds["near" if a == b else "mate" if topo.mates(a, b) else "plane" if topo.same_plane(a, b) else "two"].append((d, c))
+        kinds["N" if a == b else "M" if topo.mates(a, b) else "P" if topo.same_plane(a, b) else "T"].append((d, c))
+    return kinds
+
+
+def transfers(core, cores, topo, plan):
+    kinds = destinations(core, cores, topo)
     free = [h for h in topo.cores_of(core) if h not in cores and topo.die(h) == topo.die(core)]
-    hm = [h for h in free if topo.may_write(h, kinds["mate"][0][1])][0]
-    hs = [h for h in free if h != hm and topo.may_write(h, kinds["plane"][0][1])][0]
-    return kinds, {"mate": hm, "plane": hs}
+    x = [h for h in free if topo.may_write(h, kinds["M"][0][1])][0]
+    hand = dict(zip("xyz", [x] + [h for h in free if h != x]))
+    every = topo.engines(core, kinds["N"][0][1])
+    off = topo.engines(core, kinds["T"][0][1])
+    sets = {"all": every, "off": off, "on": [e for e in every if e not in off]}
+    out = []
+    for call in plan:
+        cl = []
+        for item in call:
+            what, via, es = item.split(":")
+            blocks = kinds[what[0]] if len(what) == 1 else [kinds[what[0]][int(what[1])]]
+            name = es.rstrip("0123456789/")
+            j, n = [int(z) for z in es[len(name):].split("/")]
+            k = len(sets[name]) // n
+            cl.append((blocks, blocks[0][1] if via == "-" else hand[via], sets[name][j * k:(j + 1) * k]))
+        out.append(cl)
+    return out
 
 
-def share(src, dests, topo):
-    es = topo.engines(src, dests[0][1])
-    k = len(es) // len(dests)
-    return [(d, 1, c, es[j * k:(j + 1) * k]) for j, (d, c) in enumerate(dests)]
+def calls_of(core, cores, topo, plan):
+    if core in cores:
+        return transfers(core, cores, topo, plan)
+    for q in cores:
+        for cl in transfers(q, cores, topo, plan):
+            for blocks, c, _ in cl:
+                if c == core:
+                    es = topo.engines(core, blocks[0][1])
+                    k = len(es) // len(blocks)
+                    return [[([b], b[1], es[j * k:(j + 1) * k]) for j, b in enumerate(blocks)]]
+    return []
 
 
-def calls_of(core, cores, topo, via):
-    if core not in cores:
-        for q in cores:
-            kinds, hand = routes(q, cores, topo)
-            for k in hand:
-                if via and hand[k] == core:
-                    return [share(core, kinds[k], topo)]
-        return []
-    kinds, hand = routes(core, cores, topo)
-    off = topo.engines(core, kinds["two"][0][1])
-    near = [(d, 1, c, [e for e in topo.engines(core, c) if e not in off]) for d, c in kinds["near"]]
-    if not via:
-        return [share(core, kinds["two"] + kinds["plane"], topo), share(core, kinds["mate"], topo) + near]
-    es = topo.engines(core, hand["mate"])
-    k = len(es) // 2
-    first = [(kinds[n][0][0], 2, hand[n], es[j * k:(j + 1) * k]) for j, n in enumerate(("plane", "mate"))]
-    return [first, share(core, kinds["two"], topo) + near]
+ARRIVALS = {}
 
 
-def arrivals(core, cores, topo, via):
-    senders = set(h for q in cores for h in topo.cores_of(q))
-    return sum(len(e) for q in senders for cl in calls_of(q, cores, topo, via) for _, _, c, e in cl if c == core)
+def arrivals(core, cores, topo, plan):
+    key = str(plan)
+    if key not in ARRIVALS:
+        ARRIVALS[key] = {}
+        for q in set(h for q in cores for h in topo.cores_of(q)):
+            for cl in calls_of(q, cores, topo, plan):
+                for _, c, e in cl:
+                    ARRIVALS[key][c] = ARRIVALS[key].get(c, 0) + len(e)
+    return ARRIVALS[key][core]
 
 
 def send(g, T, topo, call, src, dst, asem, lsem):
     tr = []
-    for d, n, c, es in call:
+    for blocks, c, es in call:
         rid, pid, _ = topo.addr(c)
         tr.append(RemoteDMATransfer(dst_ids=[DstId(rid=rid, pnc=pid)], dma_engine_mask=sum(1 << e for e in es),
-                                    remote_sem=T.sem[asem], src=src(d, n), dst=dst(d, n, c)))
+                                    remote_sem=T.sem[asem], src=src(blocks[0][0], len(blocks)), dst=dst(blocks[0][0], len(blocks), c)))
     g.remote_dma_fused(tr, local_sem=T.sem[lsem])
-    return sum(len(es) for _, _, _, es in call)
+    return sum(len(es) for _, _, es in call)
 
 
 def kinds_of(t):
-    return (("m", "wm", "cm", t in VIA_M), ("h", "hw", "pp", t in VIA_H))
+    return (("m", "wm", "cm", PLAN_M[t]), ("h", "hw", "pp", PLAN_H[t]))
 
 
 def hand_on(g, core, T, topo):
     cores = list(T.cores)
     ends = []
     for t in range(NS):
-        for name, win, land, via in kinds_of(t):
-            for call in calls_of(core, cores, topo, via):
-                d0 = call[0][0]
-                g.wait_ge(T.sem["a%s%d" % (name, t)], arrivals(core, cores, topo, via))
+        for name, win, land, plan in kinds_of(t):
+            for call in calls_of(core, cores, topo, plan):
+                d0 = call[0][0][0][0]
+                g.wait_ge(T.sem["a%s%d" % (name, t)], arrivals(core, cores, topo, plan))
                 n = send(g, T, topo, call, lambda d, n: T[land][:, (2 * t + d - d0) * S:(2 * t + d - d0 + 1) * S],
                          lambda d, n, c: T["%s%d" % (win, t % 2)][:, V + (d - 1) * S:V + d * S], "a%s%d" % (name, t), "l%s%d" % (name, t))
                 ends.append(("l%s%d" % (name, t), n))
@@ -202,60 +238,48 @@ def rank_program(g, core, T, topo):
             for s_, v_ in clock[q].items():
                 clk[s_] = max(clk.get(s_, 0), v_)
         for (q, o, i) in parts:
-            if q == "g":
+            if sem == "gd0":
                 g.dma_start(o, i, allow_slow_non_contiguous=True).then_inc(T.sem[sem], 16)
             else:
                 eng[q].dma_start(o, i).then_inc(T.sem[sem], 16)
             val = bump(sem, 16)
         after("dma", rd, wr, (sem, val, clk))
 
-    def exchange(kind, src, t, make):
-        name, win, land, via = kinds_of(t)[kind]
+    def exchange(kind, src, t):
+        name, win, land, plan = kinds_of(t)[kind]
         dst, asem, lsem = "%s%d" % (win, t % 2), "a%s%d" % (name, t), "l%s%d" % (name, t)
-        calls = calls_of(core, cores, topo, via)
-        make(runs([[((d - 1) * S, (d - 1 + n) * S) for d, n, _, _ in cl] for cl in calls]))
-        for cl in calls:
-            before("g", [(src, (d - 1) * S, (d - 1 + n) * S) for d, n, _, _ in cl], [])
+        for cl in calls_of(core, cores, topo, plan):
+            before("g", [(src, (b[0][0] - 1) * S, (b[0][0] - 1 + len(b)) * S) for b, _, _ in cl], [])
             val = bump(lsem, send(g, T, topo, cl, lambda d, n: T[src][:, (d - 1) * S:(d - 1 + n) * S],
-                                  lambda d, n, c_: T[dst][:, V + (d - 1) * S:V + d * S] if c_ in cores else T[land][:, 2 * t * S:(2 * t + 2) * S],
+                                  lambda d, n, c_: T[dst][:, V + (d - 1) * S:V + d * S] if c_ in cores else T[land][:, 2 * t * S:(2 * t + n) * S],
                                   asem, lsem))
         after("dma", [(src, 0, SH)], [], (lsem, val, dict(clock["g"])))
         acc[dst] = [e for e in acc.get(dst, []) if e[0] < V]
-        acc[dst].append([V, W, (asem, bump(asem, arrivals(core, cores, topo, via)), {}), True, "dma"])
+        acc[dst].append([V, W, (asem, bump(asem, arrivals(core, cores, topo, plan)), {}), True, "dma"])
 
-    def runs(calls):
-        out = []
-        for cl in calls:
-            cur = []
-            for lo, hi in cl:
-                if cur and cur[-1][1] == lo and hi - cur[-1][0] <= 2 * S:
-                    cur[-1] = (cur[-1][0], hi)
-                else:
-                    cur.append((lo, hi))
-            out += cur
-        return out
+    kinds = destinations(core, cores, topo)
 
-    def show_m(q, ml):
-        def make(rs):
-            for lo, hi in rs:
-                gather(q, ("sm", lo, hi), ("wrot", 0, V), (ml, 256 + lo // 16, 256 + hi // 16))
-        return make
-
-    def show_h(hn, qs):
-        def make(rs):
-            if not PE_ROT:
-                gather(qs[0], ("sh", 0, 448), (hn, 0, V), ("nat", 312, 340))
-                gather(qs[1], ("sh", 448, SH), (hn, 0, V), ("nat", 340, 368))
-                dma([("s", T.shr[0:112, :], T.sh[16:128, :]), ("a", T.shr[112:128, :], T.sh[0:16, :])], [("sh", 0, SH)], [("shr", 0, SH)])
-                return
-            for j, (lo, hi) in enumerate(rs):
-                gather(qs[1] if j == 1 else qs[0], ("sh", lo, hi), (hn, 0, V), ("nat", 312 + lo // 16, 312 + hi // 16))
-                pt = ("pt%d" % j, 0, hi - lo)
+    def show(w, t, ml, hn, words):
+        if w[0] == "+":
+            exchange("mh".index(w[1]), ("sm", "shr")["mh".index(w[1])], t)
+            return
+        lo, hi = (kinds[w[1]][0][0] - 1) * S, kinds[w[1]][-1][0] * S
+        pt = ("pn%d" % "MPTN".index(w[1]), 0, hi - lo)
+        if w[0] == "g":
+            before(w[2], [("wrot", V, 2 * V)], [])
+            gather(w[2], ("sm", lo, hi), ("wrot", 0, V), (ml, 256 + lo // 16, 256 + hi // 16))
+            after(w[2], [("wrot", V, 2 * V)], [], acc["wrot"][-1][2])
+        elif w[0] == "G":
+            gather(w[2], ("sh", lo, hi), (hn, 0, V), ("nat", 312 + lo // 16, 312 + hi // 16))
+            if "K%ss" % w[1] not in words:
                 op("t", [("rot", 0, 128), ("sh", lo, hi)], [pt], lambda: g.tensor.matmul(c(*pt), T.rot[:, :], c("sh", lo, hi), True, True))
-            for j, (lo, hi) in enumerate(rs):
-                pt = ("pt%d" % j, 0, hi - lo)
-                op("a", [pt], [("shr", lo, hi)], lambda: g.scalar.activation(c("shr", lo, hi), c(*pt), F.Copy))
-        return make
+        elif w[2] == "s":
+            dma([("s", T.shr[0:112, lo:hi], T.sh[16:128, lo:hi]), ("s", T.shr[112:128, lo:hi], T.sh[0:16, lo:hi])],
+                [("sh", lo, hi)], [("shr", lo, hi)])
+        elif w[2] == "a":
+            op("a", [pt], [("shr", lo, hi)], lambda: g.scalar.activation(c("shr", lo, hi), c(*pt), F.Copy))
+        else:
+            cp(("shr", lo, hi), pt)
 
     def c(b, lo, hi):
         return T[b][:, lo:hi]
@@ -281,39 +305,50 @@ def rank_program(g, core, T, topo):
     def gtt(out, win, off, b, o):
         op("v", [win, off, b], [out], lambda: g.vector.tensor_tensor(c(*out), c(*win).indirect(c(*off)), c(*b), o))
 
-    def pieces():
-        cp(("xx", 0, 256), ("qq", 0, 256))
-        tt(("xx", 256, 512), ("qq", 0, 256), ("xx", 0, 256), sub)
+    def moved(j, wrapq):
+        x = T.xx
+        dma([("s", T.wrot[r:112:16, :], x[16:128, r, :]) for r in (2 * j, 2 * j + 1)]
+            + [(wrapq, T.wrot[112 + r:113 + r, :], x[0:16, r, :]) for r in (2 * j, 2 * j + 1)],
+            [("xx", 256 * j, 256 * j + 256)], [("wrot", V * j, V * j + V)])
 
     def unlist(wm):
-        x = T.xx
-        dma([("s", T.wrot[r:112:16, 0:V], x[16:128, r * 128:(r + 1) * 128]) for r in range(4)]
-            + [("a", T.wrot[112 + r:113 + r, 0:V], x[0:16, r * 128:(r + 1) * 128]) for r in range(4)],
-            [("xx", 0, 512)], [("wrot", 0, V)])
-        dma([("s", T[wm][r:128:16, 0:V], x[:, r * 128:(r + 1) * 128]) for r in range(4)], [("xx", 0, 512)], [(wm, 0, V)])
+        dma([("s", T[wm][r:128:16, 0:V], T.xx[:, r, :]) for r in range(4)], [("xx", 0, 512)], [(wm, 0, V)])
+
+    def high(q, src, lo, hi, j=0):
+        o = T.xx[:, 2 * j:2 * j + 2, lo:hi]
+        op(q, [src], [("xx", 256 * j + 2 * lo, 256 * j + 2 * hi)],
+           lambda: g.vector.tensor_copy(o, c(*src)) if q == "v" else g.scalar.activation(o, c(*src), F.Copy))
+
+    def low(src, lo, hi):
+        op("v", [src, ("xx", 2 * lo, 2 * hi)], [("xx", 256 + 2 * lo, 256 + 2 * hi)],
+           lambda: g.vector.tensor_tensor(T.xx[:, 2:4, lo:hi], c(*src), T.xx[:, 0:2, lo:hi], sub))
 
     LC = [0, 128, 64, 192]
+    PA = [("pa0", 0, 64), ("pa1", 0, 64), ("pa2", 0, 64), ("pa0", 64, 128)]
 
     dma([("s", c("mi", 0, 128), T.mm[:]), ("a", c("mi", 128, 256), T.mt[:])], [], [("mi", 0, 256)])
     dma([("s", T.li[0:112, 256:312], T.sn[16:128, :]), ("a", T.li[112:128, 256:312], T.sn[0:16, :]),
          ("a", c("li", 312, 368), T.sn[:])], [], [("li", 256, 368)])
-    dma([("s", c("hw0", 0, V // 2), T.h0[:, 0:V // 2])], [], [("hw0", 0, V // 2)])
     dma([("s", c("li", 0, 256), T.pd[:]), ("a", c("lbi", 0, 256), T.lb[:]), ("a", c("ob", 0, 4), T.obs[:])], [],
         [("li", 0, 256), ("lbi", 0, 256), ("ob", 0, 4)])
+    dma([("s", c("hw0", 0, H0), T.h0[:, 0:H0])], [], [("hw0", 0, H0)])
     op("g", [], [("pi", 0, 1)], lambda: g.iota(c("pi", 0, 1), [[0, 1]], 0, 1))
     op("g", [], [("pi", 3, 4)], lambda: g.iota(c("pi", 3, 4), [[0, 1]], 112, 1))
     op("g", [], [("jr", 0, 144)], lambda: g.iota(c("jr", 0, 144), [[1, 144]], 0, 0, allow_small_or_imprecise_dtypes=True))
-    op("g", [], [("vi", 0, 64)], lambda: g.iota(c("vi", 0, 64), [[16, 64]], 0, 1, allow_small_or_imprecise_dtypes=True))
+    op("g", [], [("vi", 0, 64)], lambda: g.iota(c("vi", 0, 64), [[16, 64]], 512, 1, allow_small_or_imprecise_dtypes=True))
     dma([("g", c("tc", 0, 1), T.th[:])], [], [("tc", 0, 4)], sem="gd0")
-    op("v", [], [("wrot", 0, V)], lambda: g.vector.memset(c("wrot", 0, V), 0.0))
+    op("v", [], [("wrot", 0, 2 * V)], lambda: g.vector.memset(c("wrot", 0, V), 0.0))
     op("v", [], [("wm0", 0, V)], lambda: g.vector.memset(c("wm0", 0, V), 0.0))
     ts(("mi", 0, 128), ("mi", 0, 128), 1023, None, band)
-    cp(("qq", 0, 256), ("mi", 0, 256))
-    pieces()
+    cp(("ps", 0, 256), ("mi", 0, 256))
+    high("v", ("ps", 0, 256), 0, 128)
+    moved(0, "a")
+    low(("ps", 0, 256), 0, 128)
+    moved(1, "a")
     cp(("nat", 256, 368), ("li", 256, 368))
-    unlist("wm0")
-    dma([("s", c("hw0", V // 2, V), T.h0[:, V // 2:V])], [], [("hw0", V // 2, V)])
-    dma([("s", c("tw", 0, V), T.wv[:, 0:V])], [], [("tw", 0, V)])
+    op("a", [("wm0", 0, V)], [("wm1", 0, V)], lambda: g.scalar.activation(c("wm1", 0, V), c("wm0", 0, V), F.Copy))
+    dma([("s", c("hw0", H0, V), T.h0[:, H0:V])], [], [("hw0", H0, V)])
+    dma([("s", c("tw", 0, WV), T.wv[:, 0:WV])], [], [("tw", 0, WV)])
     ts(("pi", 3, 4), ("pi", 3, 4), 127, None, band)
     ts(("pi", 1, 2), ("pi", 0, 1), 112, None, band)
     ts(("pi", 2, 3), ("pi", 0, 1), 13, None, band)
@@ -325,170 +360,205 @@ def rank_program(g, core, T, topo):
     ts(("pc", 5, 6), ("pc", 2, 3), 1.0, None, AluOpType.is_equal)
     ts(("ec", 0, 144), ("jr", 0, 144), c("pc", 3, 4), None, AluOpType.is_equal, extra=[("pc", 3, 4)])
     ts(("idn", 0, 128), ("jr", 0, 128), c("pc", 0, 1), None, AluOpType.is_equal, extra=[("pc", 0, 1)])
-    exchange(0, "sm", 0, show_m("v", "nat"))
-    exchange(1, "shr", 0, show_h("hw0", "aa"))
-    dma([("a", c("tw", V, A), T.wv[:, V:A])], [], [("tw", V, A)])
     ts(("ex", 0, 144), ("ec", 0, 144), c("pc", 4, 5), None, mul, extra=[("pc", 4, 5)])
     ts(("em", 0, 144), ("ec", 0, 144), c("pc", 5, 6), None, mul, extra=[("pc", 5, 6)])
     cp(("nat", 0, 256), ("li", 0, 256))
     cp(("lbf", 0, 256), ("lbi", 0, 256))
-    ts(("y8", 0, 4), ("ob", 0, 4), 0.125, None, mul)
     cp(("lbh", 0, 256), ("lbf", 0, 256))
+    for w in FIRST.split():
+        if w == "*o":
+            unlist("wm0")
+        elif w == "*d":
+            op("a", [("tw", 0, WV)], [("tw", A, A + WV)], lambda: g.scalar.activation(c("tw", A, A + WV), c("tw", 0, WV), F.Copy))
+        elif w == "*g":
+            g.sem_inc(T.sem["go"], 1)
+            g.sync.wait_ge(T.sem["go"], 1)
+        elif w == "*w":
+            dma([("s", c("tw", WV, A), T.wv[:, WV:A])], [], [("tw", WV, A)])
+        else:
+            show(w, 0, "nat", "hw0", FIRST.split())
+    ts(("y8", 0, 4), ("ob", 0, 4), 0.125, None, mul)
     ts(("nt", 0, 1), ("tc", 0, 1), -1.0, None, mul)
     tt(("lbl", 0, 256), ("lbf", 0, 256), ("lbh", 0, 256), sub)
     for h in range(2):
-        ts(("kk", 128 * h, 128 * h + 64), ("vi", 0, 64), c("pc", 1, 2), 1.0 / 1024, sub, mul, extra=[("pc", 1, 2)])
-        ts(("kk", 128 * h + 64, 128 * h + 128), ("li", 64 * h, 64 * h + 64), 1.0 / 1024, None, mul)
-    tt(("f1", 0, 128), ("li", 128, 256), ("li", 0, 128), sub)
-    op("v", [], [("wm1", 0, V)], lambda: g.vector.memset(c("wm1", 0, V), 0.0))
-    ts(("dpd", 0, 128), ("f1", 0, 128), 1.0 / 1024, None, mul)
-    ts(("t1", 0, 312), ("li", 0, 312), 15, None, band)
-    ts(("t2", 0, 312), ("li", 0, 312), 4, None, shr_)
-    ts(("f1", 0, 312), ("t1", 0, 312), 128.0, None, mul)
-    ts(("f3", 0, 312), ("li", 0, 312), float(V), None, AluOpType.is_ge)
-    tt(("f1", 0, 312), ("f1", 0, 312), ("t2", 0, 312), add)
-    tt(("f2", 0, 312), ("li", 0, 312), ("f1", 0, 312), sub)
-    tt(("f2", 0, 312), ("f2", 0, 312), ("f3", 0, 312), mul)
-    tt(("f1", 0, 312), ("f1", 0, 312), ("f2", 0, 312), add)
-    cp(("tw", A, A + V), ("tw", 0, V))
-    cp(("per", 0, 312), ("f1", 0, 312))
-    cp(("tw", A + V, 2 * A), ("tw", V, A))
+        ts(("kk", 128 * h, 128 * h + 64), ("vi", 0, 64), c("pc", 1, 2), 2.0, sub, mul, extra=[("pc", 1, 2)])
+        tt(("kk", 128 * h + 64, 128 * h + 128), ("li", 64 * h, 64 * h + 64), ("li", 128 + 64 * h, 192 + 64 * h), add)
+    tt(("ps", 384, 512), ("li", 128, 256), ("li", 0, 128), sub)
+    cp(("kh", 0, 256), ("kk", 0, 256))
+    tt(("kl", 0, 256), ("kk", 0, 256), ("kh", 0, 256), sub)
+    for name, f in (("hi", 0.5), ("ni", -0.5), ("oi", 1.0), ("hi2", 0.5), ("ni2", -0.5), ("oi2", 1.0), ("i512", 512.0)):
+        ts((name, 0, 128), ("idn", 0, 128), f, None, mul)
+    op("v", [("idn", 0, 128)], [("x2", 1, 2), ("x2", 5, 6)],
+       lambda: g.vector.tensor_scalar(T.x2[:, 1:8:4, :], c("idn", 0, 128), 0.0, None, mul))
+    ts(("t2", 0, 312), ("li", 0, 312), float(V), None, AluOpType.min)
+    ts(("t1", 0, 312), ("t2", 0, 312), 15, None, band)
+    ts(("t2", 0, 312), ("t2", 0, 312), 4, 127, shr_, band)
+    ts(("f1", 0, 312), ("t1", 0, 312), 127.0, None, mul)
+    ts(("ps", 0, 312), ("t2", 0, 312), -15.0, None, mul)
+    tt(("ps", 0, 312), ("ps", 0, 312), ("f1", 0, 312), add)
+    tt(("ps", 0, 312), ("ps", 0, 312), ("li", 0, 312), add)
+    cp(("per", 0, 312), ("ps", 0, 312))
+    cp(("tw", A + WV, 2 * A), ("tw", WV, A))
 
-    def listmm(out, lo, n, wt, src, slo, start, stop, pre=()):
+    def listmm(out, wt, src, slo, start, stop, pre=()):
         fns = list(pre)
         for i in range(16):
-            fns.append(lambda i=i: g.tensor.matmul(T[out][:, lo:lo + n], T[wt][:, 15 - i:143 - i],
-                                                   T[src][:, slo + i:slo + 16 * n:16], start and i == 0, stop and i == 15))
-        rd = [(wt, 0, 144), (src, slo, slo + 16 * n)]
+            fns.append(lambda i=i: g.tensor.matmul(c(*out), T[wt][:, 15 - i:143 - i], T[src][:, slo + i:slo + 1024:16],
+                                                   start and i == 0, stop and i == 15))
+        rd = [(wt, 0, 144), (src, slo, slo + 1024)]
         if pre:
             rd += [("idn", 0, 128), ("lbh", 0, 256), ("lbl", 0, 256)]
-        op("t", rd, [(out, lo, lo + n)], *fns)
+        op("t", rd, [out], *fns)
+
+    def xq(j, n=1):
+        return ("xq", j, j + n)
+
+    def mm(items):
+        op("t", [(i[1], 0, 128) for i in items] + [i[2] for i in items], [i[0] for i in items],
+           *[lambda i=i: g.tensor.matmul(c(*i[0]), T[i[1]][:, :], c(*i[2]), i[3], i[4]) for i in items])
+
+    def act(out, in_, func, **kw):
+        op("a", [in_], [out], lambda: g.scalar.activation(c(*out), c(*in_), func, **kw))
+
+    def turn():
+        for q, rows in (("g", range(TURN)), ("a", range(TURN, 16))):
+            def one(i):
+                o, s_ = T.r2[:, i:V:16], T.r1[:, i, :]
+                return g.affine_select(o, s_, [[0, 128]], AluOpType.is_ge, 0.0, 0, 0) if q == "g" else g.scalar.activation(o, s_, F.Copy)
+            op(q, [("r1", 0, 2)], [("r2", "ga".index(q), "ga".index(q) + 1)], *[lambda i=i: one(i) for i in rows])
+        dma([("a", T.ymm[:], T.r2[0:8, :]), ("a", T.ymt[:], T.r2[8:16, :])], [("r2", 0, 2)], [])
 
     for t in range(NS):
         last = t == NS - 1
         hw, hn = "hw%d" % (t % 2), "hw%d" % ((t + 1) % 2)
         wm, wn = "wm%d" % (t % 2), "wm%d" % ((t + 1) % 2)
         ml = "nat" if t == 0 else "per"
-
-        def gm(q, k):
-            gather(q, ("mp", 1024 * k, 1024 * k + 1024), (wm, 0, W), (ml, LC[k], LC[k] + 64))
-            pt = "pt%d" % k
-            listmm(pt, 0, 64, "ex", "mp", 1024 * k, False, True, pre=[
-                lambda: g.tensor.matmul(c(pt, 0, 64), T.idn[:, :], c("lbh", LC[k], LC[k] + 64), True, False),
-                lambda: g.tensor.matmul(c(pt, 0, 64), T.idn[:, :], c("lbl", LC[k], LC[k] + 64), False, False)])
-
-        def cvt(k):
-            cp(("al", 64 * k, 64 * k + 64), ("pt%d" % k, 0, 64))
-
-        def gw(q, k):
-            gather(q, ("wa", 1024 * k, 1024 * k + 1024), ("tw", 0, 2 * A), ("al", 64 * k, 64 * k + 64))
-
-        def prod(k):
-            r = (1024 * k, 1024 * k + 1024)
-            gtt(("pp",) + r, (hw, 0, W), ("nat", LC[k], LC[k] + 64), ("wa",) + r, mul)
-
-        def absd(k):
-            r = (1024 * k, 1024 * k + 1024)
-            op("a", [("pp",) + r, ("ob", 0, 4)], [("ab",) + r],
-               lambda: g.scalar.activation(c("ab", *r), c("pp", *r), F.Abs, bias=c("ob", t, t + 1), scale=-1.0))
-            if k in ASSIST:
+        words = (LAST if last else STEP).split()
+        xb, two = ("xq", "") if last else ("x2", "2")
+        for w in words:
+            x = w[0]
+            if x in "gGK+":
+                show(w, t + 1, "per", hn, words)
+                continue
+            if x in "euw":
+                a_, b_ = [int(z) for z in w[-3:].split("-")]
+                h, lo, hi = a_ // 4, 256 * a_, 256 * b_ + 256
+                l1 = ("lst", 128 * h + (lo - 1024 * h) // 16, 128 * h + (hi - 1024 * h) // 16)
+                if x == "e":
+                    o, win = ("ee", lo, hi), ("pp", 2048 * h, 2048 * h + 2048)
+                    if w[1] == "a":
+                        op("a", [win, l1, ("y8", 0, 4)], [o], lambda: g.scalar.activation(
+                            c(*o), c(*win).indirect(c(*l1)), F.Identity, bias=c("y8", t, t + 1), scale=-0.125))
+                    else:
+                        op("v", [win, l1, ("y8", 0, 4)], [o], lambda: g.vector.tensor_scalar(
+                            c(*o), c(*win).indirect(c(*l1)), -0.125, c("y8", t, t + 1), mul, add))
+                elif x == "u":
+                    gtt(("uu", lo, hi), ("wa", 2048 * h, 2048 * h + 2048), l1, ("ee", lo, hi), mul)
+                else:
+                    gtt((hn, lo, hi), (hw, 0, W), ("lst", l1[1] + 64, l1[2] + 64), ("uu", lo, hi), add)
+                    if last:
+                        dma([("s", T.yh[:, lo:hi], c(hn, lo, hi))], [(hn, lo, hi)], [])
+                continue
+            k = int(w[1])
+            if x in "ABCDSE":
+                j, n = (int(w[-1]), 512) if "." in w else (0, 1024)
+                r = (1024 * k + 512 * j, 1024 * k + 512 * j + n)
+                l0, l1 = 32 * j, 32 * j + n // 16
+            p0, p1, sg = "pn%d" % (2 * k), "pn%d" % (2 * k + 1), ("sg", 64 * k, 64 * k + 64)
+            pn = ("pn%d" % k, 64 - 64 * (k % 2), 128 - 64 * (k % 2))
+            sums = [(p0, 0)] + ([("pa%d" % k, 128)] if "H%d" % k in words else [])
+            if x == "A":
+                gather(w[2], ("mp",) + r, (wm, 0, W), (ml, LC[k] + l0, LC[k] + l1))
+            elif x == "X":
+                listmm(PA[k], "ex", "mp", 1024 * k, False, True, pre=[
+                    lambda: g.tensor.matmul(c(*PA[k]), T.idn[:, :], c("lbh", LC[k], LC[k] + 64), True, False),
+                    lambda: g.tensor.matmul(c(*PA[k]), T.idn[:, :], c("lbl", LC[k], LC[k] + 64), False, False)])
+            elif x == "Y":
+                listmm(pn, "em", "mp", 1024 * k, True, False)
+            elif x == "Z":
+                listmm(pn, "ec", "cm", 1024 * k, False, k % 2 == 0 or words.index("N%d" % (k // 2)) < words.index(w))
+            elif x == "o":
+                cp(("al", 64 * k, 64 * k + 64), PA[k])
+            elif x == "i":
+                if k == 0:
+                    cp(("ti", 0, 256), ("al", 0, 256))
+                elif k == 1:
+                    ts(("ti", 0, 256), ("ti", 0, 256), A - 1 if last else 1023, None, band)
+                else:
+                    op("v", [("ti", 0, 256)], [(xb, j, j + 1) for j in (0, 2, 4, 6)],
+                       lambda: g.vector.tensor_copy(T[xb][:, 0:8:2, :], c("ti", 0, 256)))
+            elif x == "B":
+                gather(w[2], ("wa",) + r, ("tw", 0, 2 * A), ("al", 64 * k + l0, 64 * k + l1))
+            elif x == "C":
+                gtt(("pp",) + r, (hw, 0, W), ("nat", LC[k] + l0, LC[k] + l1), ("wa",) + r, mul)
+            elif x == "D":
+                op("a", [("pp",) + r, ("ob", 0, 4)], [("ab",) + r],
+                   lambda: g.scalar.activation(c("ab", *r), c("pp", *r), F.Abs, bias=c("ob", t, t + 1), scale=-1.0))
+            elif x == "S":
                 op("a", [("ab",) + r, ("nt", 0, 1)], [("df",) + r],
                    lambda: g.scalar.activation(c("df", *r), c("ab", *r), F.Identity, bias=c("nt", 0, 1), scale=1.0))
-
-        def comp(k):
-            r = (1024 * k, 1024 * k + 1024)
-            if k in ASSIST:
-                ts(("cm",) + r, ("df",) + r, 0.0, None, AluOpType.is_gt)
-            else:
-                ts(("cm",) + r, ("ab",) + r, c("tc", 0, 1), None, AluOpType.is_gt, extra=[("tc", 0, 1)])
-            listmm("pn%d" % (k // 2), 64 * (k % 2), 64, "ec", "cm", 1024 * k, False, k % 2 == 1)
-
-        def decide(h, with_pieces):
-            pn = "pn%d" % h
-            n1 = ("n1", 64 * h, 64 * h + 64)
-            cp(n1, (pn, 64, 128))
-            tt(("ps", 0, 64), (pn, 0, 64), n1, AluOpType.is_gt)
-            tt(("qq", 128 + 64 * h, 192 + 64 * h), (pn, 0, 64), n1, AluOpType.min)
-            tt(("ps", 128, 192), ("ps", 0, 64), ("dx", 64 * h, 64 * h + 64), mul)
-            tt(("ps", 64, 128), ("ps", 0, 64), ("dpd", 64 * h, 64 * h + 64), mul)
-            tt(("qq", 64 * h, 64 * h + 64), ("ps", 128, 192), ("xi", 128 * h, 128 * h + 64), add)
-            tt(("ps", 256, 384), ("ps", 0, 128), ("kk", 128 * h, 128 * h + 128), add)
-            if with_pieces:
-                cp(("xx", 0, 256), ("qq", 0, 256))
-            ts(("lst", 128 * h, 128 * h + 128), ("ps", 256, 384), 1024.0, None, mul)
-            if with_pieces:
-                tt(("xx", 256, 512), ("qq", 0, 256), ("xx", 0, 256), sub)
-
-        def err(h, lo, n):
-            o = ("ee", 1024 * h + lo, 1024 * h + lo + n)
-            win, off = ("pp", 2048 * h, 2048 * h + 2048), ("lst", 128 * h + lo // 16, 128 * h + (lo + n) // 16)
-            op("a", [win, off, ("y8", 0, 4)], [o],
-               lambda: g.scalar.activation(c(*o), c(*win).indirect(c(*off)), F.Identity, bias=c("y8", t, t + 1), scale=-0.125))
-
-        def upd(h, lo, n):
-            r = (1024 * h + lo, 1024 * h + lo + n)
-            gtt(("uu",) + r, ("wa", 2048 * h, 2048 * h + 2048), ("lst", 128 * h + lo // 16, 128 * h + (lo + n) // 16), ("ee",) + r, mul)
-
-        def new(h, lo, n):
-            r = (1024 * h + lo, 1024 * h + lo + n)
-            gtt((hn,) + r, (hw, 0, W), ("lst", 128 * h + 64 + lo // 16, 128 * h + 64 + (lo + n) // 16), ("uu",) + r, add)
-            if last:
-                dma([("s", T.yh[:, r[0]:r[1]], c(hn, *r))], [(hn,) + r], [])
-
-        gm("a", 0)
-        gm("v", 1)
-        gm("a", 2)
-        gm("v", 3)
-        for h in range(2):
-            listmm("pn%d" % h, 0, 128, "em", "mp", 2048 * h, True, False)
-        for w in ORDER.split():
-            k = int(w[1])
-            if w[0] == "v":
-                cvt(k)
-            elif w[0] == "i":
-                cp(("ti", 64 * k, 64 * k + 64), ("pt%d" % k, 0, 64))
-            elif w[0] == "x":
-                ts(("xi", 128 * k, 128 * k + 128), ("ti", 128 * k, 128 * k + 128), A - 1 if last else 1023, None, band)
-            elif w[0] == "y":
-                tt(("dx", 64 * k, 64 * k + 64), ("xi", 128 * k + 64, 128 * k + 128), ("xi", 128 * k, 128 * k + 64), sub)
-            elif w[0] == "w":
-                gw("a", k)
-            elif w[0] == "W":
-                gw("v", k)
-            elif w[0] == "p":
-                prod(k)
-            elif w[0] == "a":
-                absd(k)
-            elif w[0] == "c":
-                comp(k)
-            elif w[0] == "d":
-                decide(k, k == 1 and not last)
-            elif w[0] == "e":
-                err(0, 512 * k, 512)
-            elif w[0] == "u":
-                upd(0, 512 * k, 512)
-        if not last:
-            unlist(wn)
-        else:
-            dma([("s", T.ab[0:8, 0:V], c("qq", 0, 128)), ("s", T.ab[8:16, 0:V], c("qq", 128, 256))], [("qq", 0, 256)], [("ab", 0, V)])
-        err(1, 0, 1024)
-        for k in range(2):
-            if "u%d" % k not in ORDER:
-                upd(0, 512 * k, 512)
-        new(0, 0, 1024)
-        if not last:
-            exchange(0, "sm", t + 1, show_m("a", "per"))
-            upd(1, 0, 1024)
-            new(1, 0, 1024)
-            exchange(1, "shr", t + 1, show_h(hn, "va"))
-        else:
-            op("a", [("ab", 0, V)], [("ab", V, 2 * V)],
-               *[lambda i=i: g.scalar.activation(T.ab[0:16, V + i:2 * V:16], T.ab[0:16, 128 * i:128 * i + 128], F.Copy) for i in range(16)])
-            dma([("a", T.ymm[:], T.ab[0:8, V:2 * V]), ("a", T.ymt[:], T.ab[8:16, V:2 * V])], [("ab", V, 2 * V)], [])
-            upd(1, 0, 1024)
-            new(1, 0, 512)
-            new(1, 512, 256)
-            new(1, 768, 256)
+            elif x == "E":
+                if "S" + w[1:] in words or "S" + w[1] in words:
+                    ts(("cm",) + r, ("df",) + r, 0.0, None, AluOpType.is_gt)
+                else:
+                    ts(("cm",) + r, ("ab",) + r, c("tc", 0, 1), None, AluOpType.is_gt, extra=[("tc", 0, 1)])
+            elif x == "x":
+                for h in range(2):
+                    mm([(("pa2", 128 + 64 * h, 192 + 64 * h), "hi" + two, (xb, 4 * h + 2, 4 * h + 3), True, False),
+                        (("pa2", 128 + 64 * h, 192 + 64 * h), "ni" + two, (xb, 4 * h, 4 * h + 1), False, True)])
+            elif x == "n":
+                act(xq(4 * k + 1), (p0, 64, 128), F.Identity, scale=2.0)
+            elif x == "N":
+                mm([((p1, 0, 64), "ni", xq(4 * k + 1), False, words.index("Z%d" % (2 * k + 1)) < words.index(w))])
+            elif x == "Q":
+                for b, o in sums:
+                    mm([((b, o, o + 128), "hi" + two, (xb, 4 * k, 4 * k + 2), True, False),
+                        ((b, o, o + 64), "hi" + two, (xb, 4 * k + 2, 4 * k + 3), False, False)]
+                       + ([] if last else [((b, o + 64, o + 128), "hi", xq(4 * k + 1), False, False)]))
+            elif x == "s":
+                act(sg, (p1, 0, 64), F.Sign, scale=-1.0, bias=-0.5)
+            elif x == "M":
+                act(("rr",) + sg[1:], (p1, 0, 64), F.Relu, scale=-2.0)
+            elif x == "r":
+                for b, o in sums:
+                    mm([((b, o + 64, o + 128), "ni", ("rr",) + sg[1:], False, False)])
+            elif x == "t":
+                tt(("tm" + two,) + sg[1:], ("pa2", 128 + 64 * k, 192 + 64 * k), sg, mul)
+            elif x == "m":
+                for b, o in sums:
+                    mm([((b, o, o + 64), "oi" + two, ("tm" + two,) + sg[1:], False, o == 0)])
+            elif x == "h":
+                if last:
+                    act(("qq", 128 * k, 128 * k + 128), (p0, 0, 128), F.Copy)
+                else:
+                    high(w[2], (p0, 0, 128), 64 * k, 64 * k + 64)
+            elif x == "H":
+                op("t", [("nid", 0, 128), ("xx", 128 * k, 128 * k + 128)], [("pa%d" % k, 128, 256)],
+                   lambda: g.tensor.matmul(c("pa%d" % k, 128, 256), T.nid[:, :], T.xx[:, 0:2, 64 * k:64 * k + 64], False, True))
+            elif x == "l":
+                if "H%d" % k in words:
+                    high(w[2], ("pa%d" % k, 128, 256), 64 * k, 64 * k + 64, 1)
+                else:
+                    low((p0, 0, 128), 64 * k, 64 * k + 64)
+            elif x == "U":
+                if k < 2:
+                    moved(k, WRAP[k])
+                else:
+                    unlist(wn)
+            elif x == "p":
+                tt(("tp",) + sg[1:], ("ps", 384 + 64 * k, 448 + 64 * k), sg, mul)
+            elif x == "q":
+                mm([((p1, 64, 192), "hi2", ("kh", 128 * k, 128 * k + 128), True, False),
+                    ((p1, 128, 192), "hi2", ("kl", 128 * k + 64, 128 * k + 128), False, False), ((p1, 64, 128), "i512", sg, False, False),
+                    ((p1, 128, 192), "hi", ("tp",) + sg[1:], False, True)])
+            elif x == "c":
+                cp(("lst", 128 * k, 128 * k + 128), (p1, 64, 192))
+            elif x == "O":
+                qm, qM = ("qq", 128 * k, 128 * k + 64), ("qq", 128 * k + 64, 128 * k + 128)
+                dma([("sa"[k], T.r1[0:8, :, 64 * k:64 * k + 64], c(*qm)), ("sa"[k], T.r1[8:16, :, 64 * k:64 * k + 64], c(*qM))],
+                    [qm, qM], [("r1", k, k + 1)])
+            elif x == "R":
+                turn()
 
     for sem in order:
         if waited.get(sem, 0) < count[sem]:

@@ -5,58 +5,71 @@ V, S, A, NS, N = 2048, 128, 4096, 4, 8
 W = V + (N - 1) * S
 SH = (N - 1) * S
 
-HEAD = ("A0v.0 A0a.1 A1a.0 A2a.1 A1v.1 X0 o0 X1 A2v.0 o1 B0a X2 A3v.1 B1v.1 A3a.0 X3 Y3 B1a.0 Y0 o2 C0 B2a o3 D0 Y1 C1 i0 D1 C2 "
-        "Y2 S0.0 E0.1 B3a D2.0 i1 E0.0 Z0 E1 D2.1 Z1 i2 n0 S2.0 N0 M0 x0 C3 E2.0 Q0 s0 p0 q0 E2.1 Z2 c0 r0 D3 t0 "
-        "ea0-1 n1 m0 N1 E3 Z3 Q1 h0a ")
-STEP = HEAD + ("u0-1 ea2-3 l0v s1 t1 p1 M1 r1 u2-3 m1 h1a U0 l1v U1 U2 q1 c1 w0-3 ea6-7 ea4-5 u6-7 u4-5 gMa gPa gNa gTa +m "
-               "w4-7 GMv GPa GNa GTv KMa KPa KTa KNv +h")
-LAST = HEAD + "O0 u0-1 ea2-3 s1 t1 p1 M1 r1 m1 q1 w0-1 h1a O1 c1 ea4-5 u2-3 ea6-7 w2-3 u4-5 w4-5 R1 u6-7 w6-6 w7-7"
-FIRST = "*o *w gMv gPv gTv gNv +m GMa GPa KMa GTa KPa GNa KTa KNa +h *d"
+STEP = ("GMb GTa GPv GNv KTs KNs KMv KPa +h A0a.0 A0v.1 X0 A1v o0 X1 A2a B0a.0 X2 A3v o1 o2 Y3 X3 C0.0 Y2 B0a.1 B1a C0.1 o3 j0 D0.0 "
+        "j1 C1 D0.1 i0 B2a D1 B3a Y0 i1 E0 C2 Z0 n0 D2 Y1 N0 E1 Z1 s0 C3.0 C3.1 x0 p0 Q0 M0 E2 q0 D3.0 r0 Z2 c0 D3.1 ea0-1 t0 E3.a m0 "
+        "n1 E3.b Z3.a h0v N1 ea2-3 Z3.b s1 u0-1 Q1 l0v M1 t1 r1 m1 h1a p1 u2-3 U0 q1 l1v c1 w0-3 U1 U2 ea4-5 ea6-7 gMa u4-5 gPa gNa "
+        "gTa u6-7 w4-4 +m w5-7")
+LAST = ("GMb GTa KTs GPv GNv KMv KPa A0a.1 A0v.0 A1v X0 A2a o0 KNs A3v B0a +h X1 X2 o1 o2 B1a C0.0 C0.1 X3 j1 D0.0 D0.1 C1 B2a E0 Y1 "
+        "Y2 Y0 Z0 o3 i1 j0 D1 C2 Y3 B3a E1 i0 n0 C3 D2 N0 Z1 M0 s0 p0 D3 x0 q0 Q0 E2 c0 ea0-1 Z2 t0 r0 E3.a n1 Z3.a E3.b N1 u0-1 m0 "
+        "Z3.b ea2-3 Q1 s1 t1 p1 M1 r1 m1 q1 u2-3 h0a h1a c1 O0 ea4-5 O1 w0-3 u4-5 ea6-7 u6-7 R1 w4-5 w6-6 w7-7")
+FIRST = "*p *t *w kPa kMa kTa kNa gPm gMm gTm gNm +m0 +m1 *o GMa GPa KMa GTa KPa GNa KTa KNa +h0 +m2 +h1 +h2"
 P3 = [["M:x:all0/1"], ["P0:y:on0/1", "P1:z:off0/1"], ["T0:-:off0/2", "T1:-:off1/2", "N:-:on0/1"]]
-PLAN_M = [P3, P3, P3, P3]
-PLAN_H = [P3, P3, P3, P3]
+Q3 = [["P0:y:on0/1", "P1:z:off0/1"], ["M0:x:on0/1", "M1:-:off0/1"], ["T0:-:off0/2", "T1:-:off1/2", "N:-:on0/1"]]
+M0 = [["P0:y:on0/2", "P1:z:on1/2"], ["M0:-:off0/2", "M1:-:off1/2"], ["T0:-:off0/2", "T1:-:off1/2", "N:-:on0/1"]]
+H0_ = [["M:x:on0/1"], ["P0:y:on0/2", "P1:z:on1/2"], ["T0:-:off0/2", "T1:-:off1/2", "N:-:on0/1"]]
+PLAN_M = [M0, P3, P3, P3]
+PLAN_H = [H0_, P3, P3, P3]
 WV = 2048
-H0 = 768
-WRAP = "ss"
-TURN = 4
+H0 = 2048
+YB = ("pa0", "pa1")
+CUT = 10
+WC = 1024
 
 SCRATCH = {
     "rot": ("sbuf", [128, 128], "float32"),
     "hw0": ("sbuf", [128, W], "float32"), "hw1": ("sbuf", [128, W], "float32"),
     "wm0": ("sbuf", [128, W], "bfloat16"), "wm1": ("sbuf", [128, W], "bfloat16"),
-    "wrot": ("sbuf", [128, V], "bfloat16"),
+    "ff": ("sbuf", [128, 512], "bfloat16"), "fw": ("sbuf", [128, 4 * 144], "bfloat16"), "zer": ("sbuf", [128, 512], "bfloat16"),
+    "mk": ("sbuf", [128, 2 * SH], "bfloat16"), "tb": ("sbuf", [128, 16], "bfloat16"), "fl": ("sbuf", [128, 224], "uint16"),
+    "hp": ("sbuf", [128, V], "float32"), "wrot": ("sbuf", [128, V], "bfloat16"),
+    "hr": ("sbuf", [128, 128], "float32"), "nr": ("sbuf", [128, 128], "float32"),
+    "hr2": ("sbuf", [128, 128], "float16"), "or2": ("sbuf", [128, 128], "float16"), "z2": ("sbuf", [128, 128], "float16"),
+    "hi2": ("sbuf", [128, 128], "float16"), "ni2": ("sbuf", [128, 128], "float16"), "x2": ("sbuf", [128, 8, 64], "float16"),
+    "cb": ("sbuf", [128, 128], "bfloat16"),
     "tw": ("sbuf", [128, 2 * A], "bfloat16"),
     "mp": ("sbuf", [128, 4096], "bfloat16"),
     "wa": ("sbuf", [128, 4096], "float32"),
     "pp": ("sbuf", [128, 4096], "float32"),
-    "ab": ("sbuf", [128, 4096], "float32"),
+    "ab": ("sbuf", [128, 256, 16], "float32"),
     "df": ("sbuf", [128, 4096], "bfloat16"),
-    "cm": ("sbuf", [128, 4096], "bfloat16"),
+    "cm": ("sbuf", [128, 256, 16], "bfloat16"),
+    "lm": ("sbuf", [128, 2 * NS * S], "bfloat16"),
     "ee": ("sbuf", [128, V], "float32"), "uu": ("sbuf", [128, V], "float32"),
     "sh": ("sbuf", [128, SH], "float32"), "shr": ("sbuf", [128, SH], "float32"),
     "sm": ("sbuf", [128, SH], "bfloat16"),
-    "r1": ("sbuf", [16, 16, 128], "float32"), "r2": ("sbuf", [16, V], "float32"),
+    "r1": ("sbuf", [128, 512], "float32"), "r2": ("sbuf", [128, 512], "float32"),
+    "tl": ("sbuf", [128, 32], "uint16"), "ti": ("sbuf", [128, 32], "int32"),
     "li": ("sbuf", [128, 368], "int32"),
     "nat": ("sbuf", [128, 368], "uint16"), "per": ("sbuf", [128, 312], "uint16"),
     "lbi": ("sbuf", [128, 256], "int32"), "lbf": ("sbuf", [128, 256], "float32"),
     "lbh": ("sbuf", [128, 256], "bfloat16"), "lbl": ("sbuf", [128, 256], "bfloat16"),
     "mi": ("sbuf", [128, 256], "int32"),
-    "ti": ("sbuf", [128, 256], "int32"),
     "xq": ("sbuf", [128, 8, 64], "float32"),
+    "xt": ("sbuf", [128, 256], "bfloat16"),
     "sg": ("sbuf", [128, 128], "bfloat16"), "rr": ("sbuf", [128, 128], "float32"),
     "tm": ("sbuf", [128, 128], "float32"), "tp": ("sbuf", [128, 128], "float32"),
     "hi": ("sbuf", [128, 128], "float32"), "ni": ("sbuf", [128, 128], "float32"), "oi": ("sbuf", [128, 128], "float32"),
-    "nid": ("sbuf", [128, 128], "bfloat16"), "i512": ("sbuf", [128, 128], "bfloat16"),
-    "x2": ("sbuf", [128, 8, 64], "float16"), "tm2": ("sbuf", [128, 128], "float16"),
-    "hi2": ("sbuf", [128, 128], "float16"), "ni2": ("sbuf", [128, 128], "float16"), "oi2": ("sbuf", [128, 128], "float16"),
-    "kh": ("sbuf", [128, 256], "float16"), "kl": ("sbuf", [128, 256], "float16"),
-    "kk": ("sbuf", [128, 256], "float32"), "qq": ("sbuf", [128, 256], "float32"),
+    "hib": ("sbuf", [128, 128], "bfloat16"), "nib": ("sbuf", [128, 128], "bfloat16"), "i512": ("sbuf", [128, 128], "bfloat16"),
+    "tm2": ("sbuf", [128, 128], "float16"),
+    "kh": ("sbuf", [128, 256], "bfloat16"), "kl": ("sbuf", [128, 256], "bfloat16"),
+    "qq": ("sbuf", [128, 16, 16], "float32"),
     "xx": ("sbuf", [128, 4, 128], "bfloat16"),
     "al": ("sbuf", [128, 256], "uint16"), "lst": ("sbuf", [128, 256], "uint16"),
     "ob": ("sbuf", [128, 4], "float32"), "y8": ("sbuf", [128, 4], "float32"),
     "tc": ("sbuf", [128, 4], "float32"), "nt": ("sbuf", [128, 4], "float32"),
-    "pi": ("sbuf", [128, 8], "int32"), "pc": ("sbuf", [128, 8], "float32"),
-    "jr": ("sbuf", [128, 144], "float32"), "vi": ("sbuf", [128, 64], "float32"),
+    "pi": ("sbuf", [128, 8], "int32"), "pc": ("sbuf", [128, 16], "float32"),
+    "jr": ("sbuf", [128, 144], "float32"), "vi": ("sbuf", [128, 64], "float32"), "jq": ("sbuf", [128, 16], "float32"),
+    "si": ("sbuf", [128, 336], "int32"), "zf": ("sbuf", [128, 128], "float32"),
     "ec": ("sbuf", [128, 144], "bfloat16"), "ex": ("sbuf", [128, 144], "bfloat16"), "em": ("sbuf", [128, 144], "bfloat16"),
     "idn": ("sbuf", [128, 128], "bfloat16"),
     "t1": ("sbuf", [128, 312], "int32"), "t2": ("sbuf", [128, 312], "int32"),
@@ -143,7 +156,7 @@ def send(g, T, topo, call, src, dst, asem, lsem):
 
 
 def kinds_of(t):
-    return (("m", "wm", "cm", PLAN_M[t]), ("h", "hw", "pp", PLAN_H[t]))
+    return (("m", "wm", "lm", PLAN_M[t]), ("h", "hw", "pp", PLAN_H[t]))
 
 
 def hand_on(g, core, T, topo):
@@ -194,7 +207,7 @@ def rank_program(g, core, T, topo):
         toks = []
         for (lst_, w) in ((rd, False), (wr, True)):
             for (b, lo, hi) in lst_:
-                bank = SCRATCH[b][0] == "psum"
+                bank = b in SCRATCH and SCRATCH[b][0] == "psum"
                 for e in acc.get(b, []):
                     if bank and e[4] != q:
                         toks.append(e[2])
@@ -228,7 +241,7 @@ def rank_program(g, core, T, topo):
             val = bump(sem, 1)
         after(q, rd, wr, (sem, val, dict(clock[q])))
 
-    def dma(parts, rd, wr, sem=None):
+    def dma(parts, rd, wr, sem=None, add=False):
         if sem is None:
             sem = "d%d" % nd[0]
             nd[0] += 1
@@ -240,37 +253,50 @@ def rank_program(g, core, T, topo):
         for (q, o, i) in parts:
             if sem == "gd0":
                 g.dma_start(o, i, allow_slow_non_contiguous=True).then_inc(T.sem[sem], 16)
+            elif add:
+                g.dma_start(o, i, accum_op=AluOpType.add).then_inc(T.sem[sem], 16)
             else:
                 eng[q].dma_start(o, i).then_inc(T.sem[sem], 16)
             val = bump(sem, 16)
         after("dma", rd, wr, (sem, val, clk))
 
-    def exchange(kind, src, t):
+    def exchange(kind, src, t, only):
         name, win, land, plan = kinds_of(t)[kind]
         dst, asem, lsem = "%s%d" % (win, t % 2), "a%s%d" % (name, t), "l%s%d" % (name, t)
-        for cl in calls_of(core, cores, topo, plan):
+        calls = calls_of(core, cores, topo, plan)
+        for cl in (calls[int(only):int(only) + 1] if only else calls):
             before("g", [(src, (b[0][0] - 1) * S, (b[0][0] - 1 + len(b)) * S) for b, _, _ in cl], [])
             val = bump(lsem, send(g, T, topo, cl, lambda d, n: T[src][:, (d - 1) * S:(d - 1 + n) * S],
                                   lambda d, n, c_: T[dst][:, V + (d - 1) * S:V + d * S] if c_ in cores else T[land][:, 2 * t * S:(2 * t + n) * S],
                                   asem, lsem))
+        if only and int(only) < len(calls) - 1:
+            return
         after("dma", [(src, 0, SH)], [], (lsem, val, dict(clock["g"])))
         acc[dst] = [e for e in acc.get(dst, []) if e[0] < V]
         acc[dst].append([V, W, (asem, bump(asem, arrivals(core, cores, topo, plan)), {}), True, "dma"])
 
     kinds = destinations(core, cores, topo)
 
-    def show(w, t, ml, hn, words):
+    def show(w, t, hn, words):
         if w[0] == "+":
-            exchange("mh".index(w[1]), ("sm", "shr")["mh".index(w[1])], t)
+            exchange("mh".index(w[1]), ("sm", "shr")["mh".index(w[1])], t, w[2:])
             return
         lo, hi = (kinds[w[1]][0][0] - 1) * S, kinds[w[1]][-1][0] * S
         pt = ("pn%d" % "MPTN".index(w[1]), 0, hi - lo)
-        if w[0] == "g":
-            before(w[2], [("wrot", V, 2 * V)], [])
-            gather(w[2], ("sm", lo, hi), ("wrot", 0, V), (ml, 256 + lo // 16, 256 + hi // 16))
-            after(w[2], [("wrot", V, 2 * V)], [], acc["wrot"][-1][2])
+        parts = [("v", lo, lo + S), ("a", lo + S, hi)] if w[2] == "b" else [(w[2], lo, hi)]
+        if w[0] == "g" and w[2] != "m":
+            for q, l, h in parts:
+                before(q, [("wrot", V, 2 * V)], [])
+                gather(q, ("sm", l, h), ("wrot", 0, V), ("per", 256 + l // 16, 256 + h // 16))
+                after(q, [("wrot", V, 2 * V)], [], acc["wrot"][-1][2])
+        elif w[0] == "g":
+            z = min(t, 1)
+            gtt(("sm", lo, hi), ("ff", 0, 512), ("fl", 112 * z + lo // 16, 112 * z + hi // 16), ("mk", SH * z + lo, SH * z + hi), mul)
+        elif w[0] == "k":
+            gather(w[2], ("mk", lo, hi), ("tb", 0, 16), ("fl", 56 + lo // 16, 56 + hi // 16))
         elif w[0] == "G":
-            gather(w[2], ("sh", lo, hi), (hn, 0, V), ("nat", 312 + lo // 16, 312 + hi // 16))
+            for q, l, h in parts:
+                gather(q, ("sh", l, h), (hn, 0, V), ("nat", 312 + l // 16, 312 + h // 16))
             if "K%ss" % w[1] not in words:
                 op("t", [("rot", 0, 128), ("sh", lo, hi)], [pt], lambda: g.tensor.matmul(c(*pt), T.rot[:, :], c("sh", lo, hi), True, True))
         elif w[2] == "s":
@@ -282,7 +308,7 @@ def rank_program(g, core, T, topo):
             cp(("shr", lo, hi), pt)
 
     def c(b, lo, hi):
-        return T[b][:, lo:hi]
+        return T[b][:, lo // 16:hi // 16, :] if b in ("ab", "cm") else T[b][:, lo:hi]
 
     def ts(q_out, q_in, s1, s2, o0, o1=None, extra=()):
         if o1 is None:
@@ -305,14 +331,30 @@ def rank_program(g, core, T, topo):
     def gtt(out, win, off, b, o):
         op("v", [win, off, b], [out], lambda: g.vector.tensor_tensor(c(*out), c(*win).indirect(c(*off)), c(*b), o))
 
-    def moved(j, wrapq):
-        x = T.xx
-        dma([("s", T.wrot[r:112:16, :], x[16:128, r, :]) for r in (2 * j, 2 * j + 1)]
-            + [(wrapq, T.wrot[112 + r:113 + r, :], x[0:16, r, :]) for r in (2 * j, 2 * j + 1)],
+    def fold(j):
+        for bank in ("pa0", "pa1")[:2 - 2 * j]:
+            op("t", [("zer", 0, 512)], [(bank, 0, 256)],
+               lambda: g.tensor.matmul(c(bank, 0, 256), c("zer", 0, 128), c("zer", 0, 256), True, False))
+        for z in range(2):
+            bank = "pa%d" % z
+            op("t", [("fw", 0, 576), ("xx", 256 * j, 256 * j + 256)], [(bank, 0, 256)],
+               *[lambda b=b, r=r: g.tensor.matmul(c(bank, 128 * (b % 2), 128 * (b % 2) + 128), c("fw", 144 * b + 3 - r, 144 * b + 131 - r),
+                                                  T.xx[:, r, :], False, b % 2 == 1 and r == 3)
+                 for b in (2 * z, 2 * z + 1) for r in (2 * j, 2 * j + 1)])
+
+    def copy(q, out, in_):
+        if q == "v":
+            cp(out, in_)
+        else:
+            act(out, in_, F.Copy)
+
+    def moved(j):
+        dma([("s", T.wrot[r:128:16, :], T.xx[:, r, :]) for r in (2 * j, 2 * j + 1)],
             [("xx", 256 * j, 256 * j + 256)], [("wrot", V * j, V * j + V)])
 
     def unlist(wm):
-        dma([("s", T[wm][r:128:16, 0:V], T.xx[:, r, :]) for r in range(4)], [("xx", 0, 512)], [(wm, 0, V)])
+        dma([("s", T[wm][16 + r:128:16, 0:V], T.xx[0:112, r, :]) for r in range(4)]
+            + [("s", T[wm][r:r + 1, 0:V], T.xx[112:128, r, :]) for r in range(4)], [("xx", 0, 512)], [(wm, 0, V)])
 
     def high(q, src, lo, hi, j=0):
         o = T.xx[:, 2 * j:2 * j + 2, lo:hi]
@@ -324,109 +366,139 @@ def rank_program(g, core, T, topo):
            lambda: g.vector.tensor_tensor(T.xx[:, 2:4, lo:hi], c(*src), T.xx[:, 0:2, lo:hi], sub))
 
     LC = [0, 128, 64, 192]
-    PA = [("pa0", 0, 64), ("pa1", 0, 64), ("pa2", 0, 64), ("pa0", 64, 128)]
+    PA = [("pa0", 0, 64), ("pa1", 0, 64), ("pa0", 64, 128), ("pa1", 64, 128)]
 
-    dma([("s", c("mi", 0, 128), T.mm[:]), ("a", c("mi", 128, 256), T.mt[:])], [], [("mi", 0, 256)])
-    dma([("s", T.li[0:112, 256:312], T.sn[16:128, :]), ("a", T.li[112:128, 256:312], T.sn[0:16, :]),
-         ("a", c("li", 312, 368), T.sn[:])], [], [("li", 256, 368)])
-    dma([("s", c("li", 0, 256), T.pd[:]), ("a", c("lbi", 0, 256), T.lb[:]), ("a", c("ob", 0, 4), T.obs[:])], [],
-        [("li", 0, 256), ("lbi", 0, 256), ("ob", 0, 4)])
+    def act(out, in_, func, **kw):
+        op("a", [in_], [out], lambda: g.scalar.activation(c(*out), c(*in_), func, **kw))
+
+    eq = AluOpType.is_equal
+    sn_ = ("li", 256, 312)
+
+    def col(j):
+        return c("pc", j, j + 1)
+
+    def diagonal(name, f, down=0):
+        o, z = (name, 0, 128), ({"float32": "zf", "bfloat16": "zer", "float16": "z2"}[SCRATCH[name][2]], 0, 128)
+        for base in ((-down, 128 - down) if down else (0,)):
+            op("g", [z], [o], lambda: g.affine_select(c(*o), c(*z), [[-1, 128]], AluOpType.not_equal, f, base, 1))
+            z = o
+
+    dma([("s", T.mi[0:112, 0:128], T.mm[1:8, :]), ("a", T.mi[0:112, 128:256], T.mt[1:8, :]),
+         ("s", T.mi[112:128, 0:128], T.mm[0:1, :]), ("a", T.mi[112:128, 128:256], T.mt[0:1, :])], [], [("mi", 0, 256)])
+    dma([("s", T.li[0:112, 256:312], T.sn[16:128, :]), ("a", T.li[112:128, 256:312], T.sn[0:16, :])], [], [sn_])
+    dma([("a", c("li", 312, 368), T.sn[:])], [], [("li", 312, 368)])
     dma([("s", c("hw0", 0, H0), T.h0[:, 0:H0])], [], [("hw0", 0, H0)])
     op("g", [], [("pi", 0, 1)], lambda: g.iota(c("pi", 0, 1), [[0, 1]], 0, 1))
-    op("g", [], [("pi", 3, 4)], lambda: g.iota(c("pi", 3, 4), [[0, 1]], 112, 1))
-    op("g", [], [("jr", 0, 144)], lambda: g.iota(c("jr", 0, 144), [[1, 144]], 0, 0, allow_small_or_imprecise_dtypes=True))
+    op("g", [], [("jr", 0, 144)], lambda: g.iota(c("jr", 0, 144), [[1, 144]], -15, 0, allow_small_or_imprecise_dtypes=True))
+    op("g", [], [("jq", 0, 16)], lambda: g.iota(c("jq", 0, 16), [[1, 4], [0, 4]], 0, 0, allow_small_or_imprecise_dtypes=True))
+    for b, n in (("zer", 512), ("fw", 576), ("zf", 128)):
+        op("v", [], [(b, 0, n)], lambda: g.vector.memset(c(b, 0, n), 0.0))
+    for j in range(4):
+        act(("wm0", 512 * j, 512 * j + 512), ("zer", 0, 512), F.Copy)
+    for b in range(4):
+        op("g", [("zer", 0, 32)], [("fw", 144 * b, 144 * b + 144)], lambda: g.affine_select(
+            T.fw[:, 144 * b + 3:144 * b + 131:4], c("zer", 0, 32), [[-4, 32]], AluOpType.not_equal, 1.0, -b, 1))
+    diagonal("rot", 1.0, 16)
     op("g", [], [("vi", 0, 64)], lambda: g.iota(c("vi", 0, 64), [[16, 64]], 512, 1, allow_small_or_imprecise_dtypes=True))
-    dma([("g", c("tc", 0, 1), T.th[:])], [], [("tc", 0, 4)], sem="gd0")
-    op("v", [], [("wrot", 0, 2 * V)], lambda: g.vector.memset(c("wrot", 0, V), 0.0))
-    op("v", [], [("wm0", 0, V)], lambda: g.vector.memset(c("wm0", 0, V), 0.0))
-    ts(("mi", 0, 128), ("mi", 0, 128), 1023, None, band)
-    cp(("ps", 0, 256), ("mi", 0, 256))
-    high("v", ("ps", 0, 256), 0, 128)
-    moved(0, "a")
-    low(("ps", 0, 256), 0, 128)
-    moved(1, "a")
-    cp(("nat", 256, 368), ("li", 256, 368))
-    op("a", [("wm0", 0, V)], [("wm1", 0, V)], lambda: g.scalar.activation(c("wm1", 0, V), c("wm0", 0, V), F.Copy))
-    dma([("s", c("hw0", H0, V), T.h0[:, H0:V])], [], [("hw0", H0, V)])
-    dma([("s", c("tw", 0, WV), T.wv[:, 0:WV])], [], [("tw", 0, WV)])
-    ts(("pi", 3, 4), ("pi", 3, 4), 127, None, band)
+    op("g", [], [("ti", 0, 32)], lambda: g.iota(c("ti", 0, 32), [[1, 32]], 0, 32))
+    for name, f in (("idn", 1.0), ("hi", 0.5), ("ni", -0.5), ("hib", 0.5)):
+        diagonal(name, f)
     ts(("pi", 1, 2), ("pi", 0, 1), 112, None, band)
-    ts(("pi", 2, 3), ("pi", 0, 1), 13, None, band)
-    cp(("pc", 6, 7), ("pi", 3, 4))
-    cp(("pc", 0, 3), ("pi", 0, 3))
-    ts(("rot", 0, 128), ("jr", 0, 128), c("pc", 6, 7), None, AluOpType.is_equal, extra=[("pc", 6, 7)])
-    ts(("pc", 3, 4), ("pc", 1, 2), 15.0, None, add)
-    ts(("pc", 4, 5), ("pc", 2, 3), 0.0, 4.0, AluOpType.is_equal, mul)
-    ts(("pc", 5, 6), ("pc", 2, 3), 1.0, None, AluOpType.is_equal)
-    ts(("ec", 0, 144), ("jr", 0, 144), c("pc", 3, 4), None, AluOpType.is_equal, extra=[("pc", 3, 4)])
-    ts(("idn", 0, 128), ("jr", 0, 128), c("pc", 0, 1), None, AluOpType.is_equal, extra=[("pc", 0, 1)])
-    ts(("ex", 0, 144), ("ec", 0, 144), c("pc", 4, 5), None, mul, extra=[("pc", 4, 5)])
-    ts(("em", 0, 144), ("ec", 0, 144), c("pc", 5, 6), None, mul, extra=[("pc", 5, 6)])
-    cp(("nat", 0, 256), ("li", 0, 256))
-    cp(("lbf", 0, 256), ("lbi", 0, 256))
-    cp(("lbh", 0, 256), ("lbf", 0, 256))
+    ts(("pi", 2, 3), ("pi", 0, 1), 1, None, band)
+    ts(("pi", 3, 4), ("pi", 0, 1), 2, 3, shr_, band)
+    cp(("pc", 0, 4), ("pi", 0, 4))
+    ts(("tb", 0, 16), ("jq", 0, 16), col(3), None, eq, extra=[("pc", 3, 4)])
+    ts(("pc", 4, 5), ("pc", 2, 3), -4.0, 4.0, mul, add)
+    ts(("mi", 0, 128), ("mi", 0, 128), 1023, None, band)
+    cp(("ps", 128, 256), ("mi", 128, 256))
+    cp(("ps", 0, 128), ("mi", 0, 128))
+    ts(("si", 56, 112), sn_, 7, None, shr_)
+    high("v", ("ps", 0, 256), 0, 128)
+    ts(("si", 0, 56), sn_, 511, None, band)
+    fold(0)
+    low(("ps", 0, 256), 0, 128)
+    fold(1)
+    cp(("fl", 0, 112), ("si", 0, 112))
+    cp(("nat", 312, 368), ("li", 312, 368))
+    ts(("em", 0, 144), ("jr", 0, 144), col(1), col(2), eq, mul, extra=[("pc", 0, 4)])
+    ts(("ec", 0, 144), ("jr", 0, 144), col(1), None, eq, extra=[("pc", 0, 4)])
+    for z in range(2):
+        cp(("ff", 256 * z, 256 * z + 256), ("pa%d" % z, 0, 256))
     for w in FIRST.split():
         if w == "*o":
             unlist("wm0")
-        elif w == "*d":
-            op("a", [("tw", 0, WV)], [("tw", A, A + WV)], lambda: g.scalar.activation(c("tw", A, A + WV), c("tw", 0, WV), F.Copy))
-        elif w == "*g":
-            g.sem_inc(T.sem["go"], 1)
-            g.sync.wait_ge(T.sem["go"], 1)
+        elif w == "*h":
+            dma([("s", c("hw0", H0, V), T.h0[:, H0:V])], [], [("hw0", H0, V)])
+        elif w == "*p":
+            dma([("s", c("li", 0, 256), T.pd[:]), ("s", c("lbi", 0, 256), T.lb[:]), ("s", c("ob", 0, 4), T.obs[:])], [],
+                [("li", 0, 256), ("lbi", 0, 256), ("ob", 0, 4)])
+        elif w == "*t":
+            dma([("s", c("tw", 0, WV), T.wv[:, 0:WV])], [], [("tw", 0, WV)])
         elif w == "*w":
             dma([("s", c("tw", WV, A), T.wv[:, WV:A])], [], [("tw", WV, A)])
         else:
-            show(w, 0, "nat", "hw0", FIRST.split())
-    ts(("y8", 0, 4), ("ob", 0, 4), 0.125, None, mul)
-    ts(("nt", 0, 1), ("tc", 0, 1), -1.0, None, mul)
-    tt(("lbl", 0, 256), ("lbf", 0, 256), ("lbh", 0, 256), sub)
+            show(w, 0, "hw0", FIRST.split())
+    cp(("pa1", 0, 256), ("lbi", 0, 256))
+    ts(("ex", 0, 144), ("jr", 0, 144), col(1), col(4), eq, mul, extra=[("pc", 0, 5)])
+    cp(("z2", 0, 128), ("zer", 0, 128))
+    for j, keep in enumerate((1024, A)):
+        op("v", [], [("cb", 64 * j, 64 * j + 64)], lambda: g.vector.memset(c("cb", 64 * j, 64 * j + 64), 192.0 * keep))
+    cp(("nat", 0, 256), ("li", 0, 256))
+    act(("lbh", 0, 256), ("pa1", 0, 256), F.Copy)
+    act(("tw", A, A + WV), ("tw", 0, WV), F.Copy)
+    dma([("g", c("tc", 0, 1), T.th[:])], [], [("tc", 0, 4)], sem="gd0")
+    for name, f in (("hi2", 0.5), ("ni2", -0.5), ("i512", 512.0)):
+        diagonal(name, f)
+    for name, f in (("hr2", 0.5), ("hr", 0.5), ("nr", -0.5), ("or2", 1.0)):
+        diagonal(name, f, 16)
+    diagonal("oi", 1.0)
+    for b, n in (("wrot", 2 * V), ("wm1", V)):
+        op("g", [], [(b, 0, n)], lambda: g.iota(c(b, 0, V), [[0, V]], 0, 0, allow_small_or_imprecise_dtypes=True))
+    op("g", [], [("r1", 0, 512)], lambda: g.iota(c("r1", 0, 512), [[0, 512]], 0, 0, allow_small_or_imprecise_dtypes=True))
+    act(("y8", 0, 4), ("ob", 0, 4), F.Copy, scale=0.125)
+    ts(("t2", 0, 312), ("li", 0, 312), 4, None, shr_)
+    ts(("f1", 0, 312), ("li", 0, 312), 2047.0, 127.0, AluOpType.min, mul)
+    ts(("ps", 0, 312), ("t2", 0, 312), 127.0, -2047.0, AluOpType.min, mul)
     for h in range(2):
-        ts(("kk", 128 * h, 128 * h + 64), ("vi", 0, 64), c("pc", 1, 2), 2.0, sub, mul, extra=[("pc", 1, 2)])
-        tt(("kk", 128 * h + 64, 128 * h + 128), ("li", 64 * h, 64 * h + 64), ("li", 128 + 64 * h, 192 + 64 * h), add)
-    tt(("ps", 384, 512), ("li", 128, 256), ("li", 0, 128), sub)
-    cp(("kh", 0, 256), ("kk", 0, 256))
-    tt(("kl", 0, 256), ("kk", 0, 256), ("kh", 0, 256), sub)
-    for name, f in (("hi", 0.5), ("ni", -0.5), ("oi", 1.0), ("hi2", 0.5), ("ni2", -0.5), ("oi2", 1.0), ("i512", 512.0)):
-        ts((name, 0, 128), ("idn", 0, 128), f, None, mul)
-    op("v", [("idn", 0, 128)], [("x2", 1, 2), ("x2", 5, 6)],
-       lambda: g.vector.tensor_scalar(T.x2[:, 1:8:4, :], c("idn", 0, 128), 0.0, None, mul))
-    ts(("t2", 0, 312), ("li", 0, 312), float(V), None, AluOpType.min)
-    ts(("t1", 0, 312), ("t2", 0, 312), 15, None, band)
-    ts(("t2", 0, 312), ("t2", 0, 312), 4, 127, shr_, band)
-    ts(("f1", 0, 312), ("t1", 0, 312), 127.0, None, mul)
-    ts(("ps", 0, 312), ("t2", 0, 312), -15.0, None, mul)
+        ts(("pa2", 128 * h, 128 * h + 64), ("vi", 0, 64), col(1), 2.0, sub, mul, extra=[("pc", 1, 2)])
+        tt(("pa2", 128 * h + 64, 128 * h + 128), ("li", 64 * h, 64 * h + 64), ("li", 128 + 64 * h, 192 + 64 * h), add)
+    act(("kh", 0, 256), ("pa2", 0, 256), F.Copy)
+    act(("tw", A + WV, 2 * A - WC), ("tw", WV, A - WC), F.Copy)
+    cp(("tw", 2 * A - WC, 2 * A), ("tw", A - WC, A))
     tt(("ps", 0, 312), ("ps", 0, 312), ("f1", 0, 312), add)
+    tt(("lbl", 0, 256), ("pa1", 0, 256), ("lbh", 0, 256), sub)
     tt(("ps", 0, 312), ("ps", 0, 312), ("li", 0, 312), add)
+    ts(("ti", 0, 32), ("ti", 0, 32), 511, None, band)
     cp(("per", 0, 312), ("ps", 0, 312))
-    cp(("tw", A + WV, 2 * A), ("tw", WV, A))
+    cp(("tl", 0, 32), ("ti", 0, 32))
+    tt(("ps", 384, 512), ("li", 128, 256), ("li", 0, 128), sub)
+    tt(("kl", 0, 256), ("pa2", 0, 256), ("kh", 0, 256), sub)
+    op("v", [("zer", 0, 128)], [("x2", 1, 2), ("x2", 5, 6)], lambda: g.vector.tensor_copy(T.x2[:, 1:8:4, :], c("zer", 0, 128)))
 
-    def listmm(out, wt, src, slo, start, stop, pre=()):
+    def listmm(out, wt, src, slo, start, stop, pre=(), rows=range(16), book=None):
         fns = list(pre)
-        for i in range(16):
-            fns.append(lambda i=i: g.tensor.matmul(c(*out), T[wt][:, 15 - i:143 - i], T[src][:, slo + i:slo + 1024:16],
-                                                   start and i == 0, stop and i == 15))
-        rd = [(wt, 0, 144), (src, slo, slo + 1024)]
+        for i in rows:
+            x = T.cm[:, slo // 16:slo // 16 + 64, i] if src == "cm" else T[src][:, slo + i:slo + 1024:16]
+            fns.append(lambda i=i, x=x: g.tensor.matmul(c(*out), T[wt][:, 15 - i:143 - i], x, start and i == 0, stop and i == 15))
+        rd = [(wt, 0, 144), book or (src, slo, slo + 1024)]
         if pre:
-            rd += [("idn", 0, 128), ("lbh", 0, 256), ("lbl", 0, 256)]
+            rd += [("idn", 0, 128), ("lbh", 0, 256), ("lbl", 0, 256), ("cb", 0, 128)]
         op("t", rd, [out], *fns)
 
     def xq(j, n=1):
         return ("xq", j, j + n)
 
+    def xt(b, h):
+        return ("xt", 128 * b + 64 * h, 128 * b + 64 * h + 64)
+
     def mm(items):
         op("t", [(i[1], 0, 128) for i in items] + [i[2] for i in items], [i[0] for i in items],
            *[lambda i=i: g.tensor.matmul(c(*i[0]), T[i[1]][:, :], c(*i[2]), i[3], i[4]) for i in items])
 
-    def act(out, in_, func, **kw):
-        op("a", [in_], [out], lambda: g.scalar.activation(c(*out), c(*in_), func, **kw))
-
-    def turn():
-        for q, rows in (("g", range(TURN)), ("a", range(TURN, 16))):
-            def one(i):
-                o, s_ = T.r2[:, i:V:16], T.r1[:, i, :]
-                return g.affine_select(o, s_, [[0, 128]], AluOpType.is_ge, 0.0, 0, 0) if q == "g" else g.scalar.activation(o, s_, F.Copy)
-            op(q, [("r1", 0, 2)], [("r2", "ga".index(q), "ga".index(q) + 1)], *[lambda i=i: one(i) for i in rows])
-        dma([("a", T.ymm[:], T.r2[0:8, :]), ("a", T.ymt[:], T.r2[8:16, :])], [("r2", 0, 2)], [])
+    def turn(q):
+        before(q, [("r1", 512, 514)], [])
+        gather(q, ("r2", 0, 512), ("r1", 0, 512), ("tl", 0, 32))
+        dma([("a", T.ymm[:], T.r2[0:64, 0:256]), ("a", T.ymt[:], T.r2[0:64, 256:512])], [("r2", 0, 512)], [])
 
     for t in range(NS):
         last = t == NS - 1
@@ -434,13 +506,19 @@ def rank_program(g, core, T, topo):
         wm, wn = "wm%d" % (t % 2), "wm%d" % ((t + 1) % 2)
         ml = "nat" if t == 0 else "per"
         words = (LAST if last else STEP).split()
-        xb, two = ("xq", "") if last else ("x2", "2")
+        two, keep = ("", A) if last else ("2", 1024)
+        big = 192.0 * keep
+        half, nhalf, one, xb = ("hi", "ni", "oi", "xq") if last else ("hr", "nr", "or2", "x2")
         for w in words:
             x = w[0]
-            if x in "gGK+":
-                show(w, t + 1, "per", hn, words)
+            if x == "g" or w == "+m":
+                show(w, t + 1, hn, words)
                 continue
-            if x in "euw":
+            if x in "GK+":
+                if t:
+                    show(w, t, hw, words)
+                continue
+            if x in "euwvyz":
                 a_, b_ = [int(z) for z in w[-3:].split("-")]
                 h, lo, hi = a_ // 4, 256 * a_, 256 * b_ + 256
                 l1 = ("lst", 128 * h + (lo - 1024 * h) // 16, 128 * h + (hi - 1024 * h) // 16)
@@ -454,39 +532,54 @@ def rank_program(g, core, T, topo):
                             c(*o), c(*win).indirect(c(*l1)), -0.125, c("y8", t, t + 1), mul, add))
                 elif x == "u":
                     gtt(("uu", lo, hi), ("wa", 2048 * h, 2048 * h + 2048), l1, ("ee", lo, hi), mul)
+                elif x == "v":
+                    gather(w[1], ("hp", lo, hi), (hw, 0, W), ("lst", l1[1] + 64, l1[2] + 64))
+                    mm([((YB[a_ // 2], 0, hi - lo), "oi", ("hp", lo, hi), True, False)])
+                elif x == "y":
+                    mm([((YB[a_ // 2], 0, hi - lo), "oi", ("uu", lo, hi), False, True)])
+                elif x == "z":
+                    copy(w[1], (hn, lo, hi), (YB[a_ // 2], 0, hi - lo))
+                    if last:
+                        dma([("s", T.yh[:, lo:hi], c(hn, lo, hi))], [(hn, lo, hi)], [])
                 else:
                     gtt((hn, lo, hi), (hw, 0, W), ("lst", l1[1] + 64, l1[2] + 64), ("uu", lo, hi), add)
                     if last:
                         dma([("s", T.yh[:, lo:hi], c(hn, lo, hi))], [(hn, lo, hi)], [])
                 continue
             k = int(w[1])
+            if x in "EZ" and w[-2:] in (".a", ".b"):
+                rows, book = (range(CUT), ("cm", 1024 * k, 1024 * k + 1024)) if w[-1] == "a" else (range(CUT, 16), ("cm", A + k, A + k + 1))
+                if x == "E":
+                    o, i_ = (T[b][:, 64 * k:64 * k + 64, rows[0]:rows[-1] + 1] for b in ("cm", "ab"))
+                    op("v", [("ab", 1024 * k, 1024 * k + 1024), ("tc", 0, 1)], [book],
+                       lambda: g.vector.tensor_scalar(o, i_, c("tc", 0, 1), None, AluOpType.is_gt))
+                else:
+                    listmm(("pn%d" % k, 64 - 64 * (k % 2), 128 - 64 * (k % 2)), "ec", "cm", 1024 * k, False, True, rows=rows, book=book)
+                continue
             if x in "ABCDSE":
                 j, n = (int(w[-1]), 512) if "." in w else (0, 1024)
                 r = (1024 * k + 512 * j, 1024 * k + 512 * j + n)
                 l0, l1 = 32 * j, 32 * j + n // 16
             p0, p1, sg = "pn%d" % (2 * k), "pn%d" % (2 * k + 1), ("sg", 64 * k, 64 * k + 64)
             pn = ("pn%d" % k, 64 - 64 * (k % 2), 128 - 64 * (k % 2))
-            sums = [(p0, 0)] + ([("pa%d" % k, 128)] if "H%d" % k in words else [])
             if x == "A":
                 gather(w[2], ("mp",) + r, (wm, 0, W), (ml, LC[k] + l0, LC[k] + l1))
             elif x == "X":
                 listmm(PA[k], "ex", "mp", 1024 * k, False, True, pre=[
                     lambda: g.tensor.matmul(c(*PA[k]), T.idn[:, :], c("lbh", LC[k], LC[k] + 64), True, False),
-                    lambda: g.tensor.matmul(c(*PA[k]), T.idn[:, :], c("lbl", LC[k], LC[k] + 64), False, False)])
+                    lambda: g.tensor.matmul(c(*PA[k]), T.idn[:, :], c("lbl", LC[k], LC[k] + 64), False, False),
+                    lambda: g.tensor.matmul(c(*PA[k]), T.idn[:, :], c("cb", 64 * last, 64 * last + 64), False, False)])
             elif x == "Y":
                 listmm(pn, "em", "mp", 1024 * k, True, False)
             elif x == "Z":
                 listmm(pn, "ec", "cm", 1024 * k, False, k % 2 == 0 or words.index("N%d" % (k // 2)) < words.index(w))
             elif x == "o":
-                cp(("al", 64 * k, 64 * k + 64), PA[k])
+                ts(("al", 64 * k, 64 * k + 64), PA[k], -big, None, add)
             elif x == "i":
-                if k == 0:
-                    cp(("ti", 0, 256), ("al", 0, 256))
-                elif k == 1:
-                    ts(("ti", 0, 256), ("ti", 0, 256), A - 1 if last else 1023, None, band)
-                else:
-                    op("v", [("ti", 0, 256)], [(xb, j, j + 1) for j in (0, 2, 4, 6)],
-                       lambda: g.vector.tensor_copy(T[xb][:, 0:8:2, :], c("ti", 0, 256)))
+                op("v", [("pa%d" % k, 0, 128), ("xt", 128 * k, 128 * k + 128)], [(xb, j, j + 1) for j in (2 * k, 2 * k + 4)],
+                   lambda: g.vector.tensor_tensor(T[xb][:, 2 * k:8:4, :], c("pa%d" % k, 0, 128), c("xt", 128 * k, 128 * k + 128), sub))
+            elif x == "j":
+                act(("xt", 128 * k, 128 * k + 128), ("pa%d" % k, 0, 128), F.Identity, bias=-(keep - 1) / 2)
             elif x == "B":
                 gather(w[2], ("wa",) + r, ("tw", 0, 2 * A), ("al", 64 * k + l0, 64 * k + l1))
             elif x == "C":
@@ -495,6 +588,8 @@ def rank_program(g, core, T, topo):
                 op("a", [("pp",) + r, ("ob", 0, 4)], [("ab",) + r],
                    lambda: g.scalar.activation(c("ab", *r), c("pp", *r), F.Abs, bias=c("ob", t, t + 1), scale=-1.0))
             elif x == "S":
+                if "nt" not in acc:
+                    act(("nt", 0, 1), ("tc", 0, 1), F.Copy, scale=-1.0)
                 op("a", [("ab",) + r, ("nt", 0, 1)], [("df",) + r],
                    lambda: g.scalar.activation(c("df", *r), c("ab", *r), F.Identity, bias=c("nt", 0, 1), scale=1.0))
             elif x == "E":
@@ -504,61 +599,53 @@ def rank_program(g, core, T, topo):
                     ts(("cm",) + r, ("ab",) + r, c("tc", 0, 1), None, AluOpType.is_gt, extra=[("tc", 0, 1)])
             elif x == "x":
                 for h in range(2):
-                    mm([(("pa2", 128 + 64 * h, 192 + 64 * h), "hi" + two, (xb, 4 * h + 2, 4 * h + 3), True, False),
-                        (("pa2", 128 + 64 * h, 192 + 64 * h), "ni" + two, (xb, 4 * h, 4 * h + 1), False, True)])
+                    o = ("pa2", 128 + 64 * h, 192 + 64 * h)
+                    mm([(o, "hi" + two, (xb, 4 * h + 2, 4 * h + 3), True, False), (o, "ni" + two, (xb, 4 * h, 4 * h + 1), False, True)])
             elif x == "n":
                 act(xq(4 * k + 1), (p0, 64, 128), F.Identity, scale=2.0)
             elif x == "N":
-                mm([((p1, 0, 64), "ni", xq(4 * k + 1), False, words.index("Z%d" % (2 * k + 1)) < words.index(w))])
+                mm([((p1, 0, 64), "ni", xq(4 * k + 1), False, "Z%d" % (2 * k + 1) in words[:words.index(w)])])
             elif x == "Q":
-                for b, o in sums:
-                    mm([((b, o, o + 128), "hi" + two, (xb, 4 * k, 4 * k + 2), True, False),
-                        ((b, o, o + 64), "hi" + two, (xb, 4 * k + 2, 4 * k + 3), False, False)]
-                       + ([] if last else [((b, o + 64, o + 128), "hi", xq(4 * k + 1), False, False)]))
+                mm([((p0, 0, 128), half + two, (xb, 4 * k, 4 * k + 2), True, False),
+                    ((p0, 0, 64), half + two, (xb, 4 * k + 2, 4 * k + 3), False, False)]
+                   + ([] if last else [((p0, 64, 128), half, xq(4 * k + 1), False, False)]))
             elif x == "s":
                 act(sg, (p1, 0, 64), F.Sign, scale=-1.0, bias=-0.5)
             elif x == "M":
                 act(("rr",) + sg[1:], (p1, 0, 64), F.Relu, scale=-2.0)
             elif x == "r":
-                for b, o in sums:
-                    mm([((b, o + 64, o + 128), "ni", ("rr",) + sg[1:], False, False)])
+                mm([((p0, 64, 128), nhalf, ("rr",) + sg[1:], False, words.index("m%d" % k) < words.index(w))])
             elif x == "t":
                 tt(("tm" + two,) + sg[1:], ("pa2", 128 + 64 * k, 192 + 64 * k), sg, mul)
             elif x == "m":
-                for b, o in sums:
-                    mm([((b, o, o + 64), "oi" + two, ("tm" + two,) + sg[1:], False, o == 0)])
+                mm([((p0, 0, 64), one, ("tm" + two,) + sg[1:], False, words.index("r%d" % k) < words.index(w))])
             elif x == "h":
                 if last:
-                    act(("qq", 128 * k, 128 * k + 128), (p0, 0, 128), F.Copy)
+                    for j in range(2):
+                        op("a", [(p0, 0, 128)], [("qq", 2 * k + j, 2 * k + j + 1)], lambda: g.scalar.activation(
+                            T.qq[:, 8 * k + j:8 * k + 8:2, :], c(p0, 64 * j, 64 * j + 64), F.Copy))
                 else:
                     high(w[2], (p0, 0, 128), 64 * k, 64 * k + 64)
-            elif x == "H":
-                op("t", [("nid", 0, 128), ("xx", 128 * k, 128 * k + 128)], [("pa%d" % k, 128, 256)],
-                   lambda: g.tensor.matmul(c("pa%d" % k, 128, 256), T.nid[:, :], T.xx[:, 0:2, 64 * k:64 * k + 64], False, True))
             elif x == "l":
-                if "H%d" % k in words:
-                    high(w[2], ("pa%d" % k, 128, 256), 64 * k, 64 * k + 64, 1)
-                else:
-                    low((p0, 0, 128), 64 * k, 64 * k + 64)
+                low((p0, 0, 128), 64 * k, 64 * k + 64)
             elif x == "U":
                 if k < 2:
-                    moved(k, WRAP[k])
+                    moved(k)
                 else:
                     unlist(wn)
             elif x == "p":
                 tt(("tp",) + sg[1:], ("ps", 384 + 64 * k, 448 + 64 * k), sg, mul)
             elif x == "q":
-                mm([((p1, 64, 192), "hi2", ("kh", 128 * k, 128 * k + 128), True, False),
-                    ((p1, 128, 192), "hi2", ("kl", 128 * k + 64, 128 * k + 128), False, False), ((p1, 64, 128), "i512", sg, False, False),
+                mm([((p1, 64, 192), "hib", ("kh", 128 * k, 128 * k + 128), True, False),
+                    ((p1, 64, 192), "hib", ("kl", 128 * k, 128 * k + 128), False, False), ((p1, 64, 128), "i512", sg, False, False),
                     ((p1, 128, 192), "hi", ("tp",) + sg[1:], False, True)])
             elif x == "c":
                 cp(("lst", 128 * k, 128 * k + 128), (p1, 64, 192))
             elif x == "O":
-                qm, qM = ("qq", 128 * k, 128 * k + 64), ("qq", 128 * k + 64, 128 * k + 128)
-                dma([("sa"[k], T.r1[0:8, :, 64 * k:64 * k + 64], c(*qm)), ("sa"[k], T.r1[8:16, :, 64 * k:64 * k + 64], c(*qM))],
-                    [qm, qM], [("r1", k, k + 1)])
+                dma([("s", T.r1[b:64:8, :], T.qq[:, 2 * b:2 * b + 2, :]) for b in range(4 * k, 4 * k + 4)],
+                    [("qq", 2 * k, 2 * k + 2), ("r1", 0, 512)], [("r1", 512 + k, 513 + k)])
             elif x == "R":
-                turn()
+                turn("a")
 
     for sem in order:
         if waited.get(sem, 0) < count[sem]:

from concourse.bass import DstId, RemoteDMATransfer
from concourse.mybir import AluOpType, ActivationFunctionType

V, S, A, NS, N = 2048, 128, 4096, 4, 8
W = V + (N - 1) * S
SH = (N - 1) * S

STEP = ("GMb GTa GPv GNv KTs KNs KMv KPa +h A0a.0 A0v.1 X0 A1v o0 X1 A2a B0a.0 X2 A3v o1 o2 Y3 X3 C0.0 Y2 B0a.1 B1a C0.1 o3 j0 D0.0 "
        "j1 C1 D0.1 i0 B2a D1 B3a Y0 i1 E0 C2 Z0 n0 D2 Y1 N0 E1 Z1 s0 C3.0 C3.1 x0 p0 Q0 M0 E2 q0 D3.0 r0 Z2 c0 D3.1 ea0-1 t0 E3.a m0 "
        "n1 E3.b Z3.a h0v N1 ea2-3 Z3.b s1 u0-1 Q1 l0v M1 t1 r1 m1 h1a p1 u2-3 U0 q1 l1v c1 w0-3 U1 U2 ea4-5 ea6-7 gMa u4-5 gPa gNa "
        "gTa u6-7 w4-4 +m w5-7")
LAST = ("GMb GTa KTs GPv GNv KMv KPa A0a.1 A0v.0 A1v X0 A2a o0 KNs A3v B0a +h X1 X2 o1 o2 B1a C0.0 C0.1 X3 j1 D0.0 D0.1 C1 B2a E0 Y1 "
        "Y2 Y0 Z0 o3 i1 j0 D1 C2 Y3 B3a E1 i0 n0 C3 D2 N0 Z1 M0 s0 p0 D3 x0 q0 Q0 E2 c0 ea0-1 Z2 t0 r0 E3.a n1 Z3.a E3.b N1 u0-1 m0 "
        "Z3.b ea2-3 Q1 s1 t1 p1 M1 r1 m1 q1 u2-3 h0a h1a c1 O0 ea4-5 O1 w0-3 u4-5 ea6-7 u6-7 R1 w4-5 w6-6 w7-7")
FIRST = "*p *t *w kPa kMa kTa kNa gPm gMm gTm gNm +m0 +m1 *o GMa GPa KMa GTa KPa GNa KTa KNa +h0 +m2 +h1 +h2"
P3 = [["M:x:all0/1"], ["P0:y:on0/1", "P1:z:off0/1"], ["T0:-:off0/2", "T1:-:off1/2", "N:-:on0/1"]]
Q3 = [["P0:y:on0/1", "P1:z:off0/1"], ["M0:x:on0/1", "M1:-:off0/1"], ["T0:-:off0/2", "T1:-:off1/2", "N:-:on0/1"]]
M0 = [["P0:y:on0/2", "P1:z:on1/2"], ["M0:-:off0/2", "M1:-:off1/2"], ["T0:-:off0/2", "T1:-:off1/2", "N:-:on0/1"]]
H0_ = [["M:x:on0/1"], ["P0:y:on0/2", "P1:z:on1/2"], ["T0:-:off0/2", "T1:-:off1/2", "N:-:on0/1"]]
PLAN_M = [M0, P3, P3, P3]
PLAN_H = [H0_, P3, P3, P3]
WV = 2048
H0 = 2048
YB = ("pa0", "pa1")
CUT = 10
WC = 1024

SCRATCH = {
    "rot": ("sbuf", [128, 128], "float32"),
    "hw0": ("sbuf", [128, W], "float32"), "hw1": ("sbuf", [128, W], "float32"),
    "wm0": ("sbuf", [128, W], "bfloat16"), "wm1": ("sbuf", [128, W], "bfloat16"),
    "ff": ("sbuf", [128, 512], "bfloat16"), "fw": ("sbuf", [128, 4 * 144], "bfloat16"), "zer": ("sbuf", [128, 512], "bfloat16"),
    "mk": ("sbuf", [128, 2 * SH], "bfloat16"), "tb": ("sbuf", [128, 16], "bfloat16"), "fl": ("sbuf", [128, 224], "uint16"),
    "hp": ("sbuf", [128, V], "float32"), "wrot": ("sbuf", [128, V], "bfloat16"),
    "hr": ("sbuf", [128, 128], "float32"), "nr": ("sbuf", [128, 128], "float32"),
    "hr2": ("sbuf", [128, 128], "float16"), "or2": ("sbuf", [128, 128], "float16"), "z2": ("sbuf", [128, 128], "float16"),
    "hi2": ("sbuf", [128, 128], "float16"), "ni2": ("sbuf", [128, 128], "float16"), "x2": ("sbuf", [128, 8, 64], "float16"),
    "cb": ("sbuf", [128, 128], "bfloat16"),
    "tw": ("sbuf", [128, 2 * A], "bfloat16"),
    "mp": ("sbuf", [128, 4096], "bfloat16"),
    "wa": ("sbuf", [128, 4096], "float32"),
    "pp": ("sbuf", [128, 4096], "float32"),
    "ab": ("sbuf", [128, 256, 16], "float32"),
    "df": ("sbuf", [128, 4096], "bfloat16"),
    "cm": ("sbuf", [128, 256, 16], "bfloat16"),
    "lm": ("sbuf", [128, 2 * NS * S], "bfloat16"),
    "ee": ("sbuf", [128, V], "float32"), "uu": ("sbuf", [128, V], "float32"),
    "sh": ("sbuf", [128, SH], "float32"), "shr": ("sbuf", [128, SH], "float32"),
    "sm": ("sbuf", [128, SH], "bfloat16"),
    "r1": ("sbuf", [128, 512], "float32"), "r2": ("sbuf", [128, 512], "float32"),
    "tl": ("sbuf", [128, 32], "uint16"), "ti": ("sbuf", [128, 32], "int32"),
    "li": ("sbuf", [128, 368], "int32"),
    "nat": ("sbuf", [128, 368], "uint16"), "per": ("sbuf", [128, 312], "uint16"),
    "lbi": ("sbuf", [128, 256], "int32"), "lbf": ("sbuf", [128, 256], "float32"),
    "lbh": ("sbuf", [128, 256], "bfloat16"), "lbl": ("sbuf", [128, 256], "bfloat16"),
    "mi": ("sbuf", [128, 256], "int32"),
    "xq": ("sbuf", [128, 8, 64], "float32"),
    "xt": ("sbuf", [128, 256], "bfloat16"),
    "sg": ("sbuf", [128, 128], "bfloat16"), "rr": ("sbuf", [128, 128], "float32"),
    "tm": ("sbuf", [128, 128], "float32"), "tp": ("sbuf", [128, 128], "float32"),
    "hi": ("sbuf", [128, 128], "float32"), "ni": ("sbuf", [128, 128], "float32"), "oi": ("sbuf", [128, 128], "float32"),
    "hib": ("sbuf", [128, 128], "bfloat16"), "nib": ("sbuf", [128, 128], "bfloat16"), "i512": ("sbuf", [128, 128], "bfloat16"),
    "tm2": ("sbuf", [128, 128], "float16"),
    "kh": ("sbuf", [128, 256], "bfloat16"), "kl": ("sbuf", [128, 256], "bfloat16"),
    "qq": ("sbuf", [128, 16, 16], "float32"),
    "xx": ("sbuf", [128, 4, 128], "bfloat16"),
    "al": ("sbuf", [128, 256], "uint16"), "lst": ("sbuf", [128, 256], "uint16"),
    "ob": ("sbuf", [128, 4], "float32"), "y8": ("sbuf", [128, 4], "float32"),
    "tc": ("sbuf", [128, 4], "float32"), "nt": ("sbuf", [128, 4], "float32"),
    "pi": ("sbuf", [128, 8], "int32"), "pc": ("sbuf", [128, 16], "float32"),
    "jr": ("sbuf", [128, 144], "float32"), "vi": ("sbuf", [128, 64], "float32"), "jq": ("sbuf", [128, 16], "float32"),
    "si": ("sbuf", [128, 336], "int32"), "zf": ("sbuf", [128, 128], "float32"),
    "ec": ("sbuf", [128, 144], "bfloat16"), "ex": ("sbuf", [128, 144], "bfloat16"), "em": ("sbuf", [128, 144], "bfloat16"),
    "idn": ("sbuf", [128, 128], "bfloat16"),
    "t1": ("sbuf", [128, 312], "int32"), "t2": ("sbuf", [128, 312], "int32"),
    "f1": ("sbuf", [128, 312], "float32"),
    "pa0": ("psum", [128, 512], "float32"), "pa1": ("psum", [128, 512], "float32"), "pa2": ("psum", [128, 512], "float32"),
    "pn0": ("psum", [128, 512], "float32"), "pn1": ("psum", [128, 512], "float32"),
    "pn2": ("psum", [128, 512], "float32"), "pn3": ("psum", [128, 512], "float32"),
    "ps": ("psum", [128, 512], "float32"),
}
NDMA = 64
SEMAPHORES = (["cv", "ca", "ct", "cg"] + ["d%d" % i for i in range(NDMA)] + ["gd0", "gd1", "go"]
              + ["am%d" % t for t in range(NS)] + ["ah%d" % t for t in range(NS)]
              + ["lm%d" % t for t in range(NS)] + ["lh%d" % t for t in range(NS)])
COUNTER = {"v": "cv", "a": "ca", "t": "ct", "g": "cg"}


def destinations(core, cores, topo):
    r = cores.index(core)
    kinds = {"N": [], "M": [], "P": [], "T": []}
    for d in range(1, N):
        c = cores[(r + d) % N]
        a, b = topo.chip(core), topo.chip(c)
        kinds["N" if a == b else "M" if topo.mates(a, b) else "P" if topo.same_plane(a, b) else "T"].append((d, c))
    return kinds


def transfers(core, cores, topo, plan):
    kinds = destinations(core, cores, topo)
    free = [h for h in topo.cores_of(core) if h not in cores and topo.die(h) == topo.die(core)]
    x = [h for h in free if topo.may_write(h, kinds["M"][0][1])][0]
    hand = dict(zip("xyz", [x] + [h for h in free if h != x]))
    every = topo.engines(core, kinds["N"][0][1])
    off = topo.engines(core, kinds["T"][0][1])
    sets = {"all": every, "off": off, "on": [e for e in every if e not in off]}
    out = []
    for call in plan:
        cl = []
        for item in call:
            what, via, es = item.split(":")
            blocks = kinds[what[0]] if len(what) == 1 else [kinds[what[0]][int(what[1])]]
            name = es.rstrip("0123456789/")
            j, n = [int(z) for z in es[len(name):].split("/")]
            k = len(sets[name]) // n
            cl.append((blocks, blocks[0][1] if via == "-" else hand[via], sets[name][j * k:(j + 1) * k]))
        out.append(cl)
    return out


def calls_of(core, cores, topo, plan):
    if core in cores:
        return transfers(core, cores, topo, plan)
    for q in cores:
        for cl in transfers(q, cores, topo, plan):
            for blocks, c, _ in cl:
                if c == core:
                    es = topo.engines(core, blocks[0][1])
                    k = len(es) // len(blocks)
                    return [[([b], b[1], es[j * k:(j + 1) * k]) for j, b in enumerate(blocks)]]
    return []


ARRIVALS = {}


def arrivals(core, cores, topo, plan):
    key = str(plan)
    if key not in ARRIVALS:
        ARRIVALS[key] = {}
        for q in set(h for q in cores for h in topo.cores_of(q)):
            for cl in calls_of(q, cores, topo, plan):
                for _, c, e in cl:
                    ARRIVALS[key][c] = ARRIVALS[key].get(c, 0) + len(e)
    return ARRIVALS[key][core]


def send(g, T, topo, call, src, dst, asem, lsem):
    tr = []
    for blocks, c, es in call:
        rid, pid, _ = topo.addr(c)
        tr.append(RemoteDMATransfer(dst_ids=[DstId(rid=rid, pnc=pid)], dma_engine_mask=sum(1 << e for e in es),
                                    remote_sem=T.sem[asem], src=src(blocks[0][0], len(blocks)), dst=dst(blocks[0][0], len(blocks), c)))
    g.remote_dma_fused(tr, local_sem=T.sem[lsem])
    return sum(len(es) for _, _, es in call)


def kinds_of(t):
    return (("m", "wm", "lm", PLAN_M[t]), ("h", "hw", "pp", PLAN_H[t]))


def hand_on(g, core, T, topo):
    cores = list(T.cores)
    ends = []
    for t in range(NS):
        for name, win, land, plan in kinds_of(t):
            for call in calls_of(core, cores, topo, plan):
                d0 = call[0][0][0][0]
                g.wait_ge(T.sem["a%s%d" % (name, t)], arrivals(core, cores, topo, plan))
                n = send(g, T, topo, call, lambda d, n: T[land][:, (2 * t + d - d0) * S:(2 * t + d - d0 + 1) * S],
                         lambda d, n, c: T["%s%d" % (win, t % 2)][:, V + (d - 1) * S:V + d * S], "a%s%d" % (name, t), "l%s%d" % (name, t))
                ends.append(("l%s%d" % (name, t), n))
    for sem, n in ends:
        g.wait_ge(T.sem[sem], n)


def rank_program(g, core, T, topo):
    rank = T.rank_of(core)
    if rank is None:
        hand_on(g, core, T, topo)
        return
    cores = list(T.cores)
    add, sub, mul = AluOpType.add, AluOpType.subtract, AluOpType.mult
    band, shr_ = AluOpType.bitwise_and, AluOpType.logical_shift_right
    F = ActivationFunctionType
    eng = {"v": g.vector, "a": g.scalar, "t": g.tensor, "s": g.sync, "g": g}

    clock = {q: {} for q in eng}
    count = {}
    waited = {}
    order = []
    acc = {}
    nd = [0]

    def need(q, tok):
        sem, val, clk = tok
        if clock[q].get(sem, 0) >= val:
            return
        eng[q].wait_ge(T.sem[sem], val)
        waited[sem] = max(waited.get(sem, 0), val)
        for s_, v_ in clk.items():
            if clock[q].get(s_, 0) < v_:
                clock[q][s_] = v_
        clock[q][sem] = val

    def before(q, rd, wr):
        toks = []
        for (lst_, w) in ((rd, False), (wr, True)):
            for (b, lo, hi) in lst_:
                bank = b in SCRATCH and SCRATCH[b][0] == "psum"
                for e in acc.get(b, []):
                    if bank and e[4] != q:
                        toks.append(e[2])
                    elif e[0] < hi and lo < e[1] and (w or e[3]) and not (q == "t" and e[4] == "t"):
                        toks.append(e[2])
        best = {}
        for tk in toks:
            if tk[0] not in best or best[tk[0]][1] < tk[1]:
                best[tk[0]] = tk
        for tk in sorted(best.values(), key=lambda x: -len(x[2])):
            need(q, tk)

    def after(q, rd, wr, tok):
        for (b, lo, hi) in wr:
            acc[b] = [e for e in acc.get(b, []) if not (lo <= e[0] and e[1] <= hi)]
            acc[b].append([lo, hi, tok, True, q])
        for (b, lo, hi) in rd:
            acc.setdefault(b, []).append([lo, hi, tok, False, q])

    def bump(sem, n):
        count[sem] = count.get(sem, 0) + n
        if sem not in order:
            order.append(sem)
        return count[sem]

    def op(q, rd, wr, *fns):
        before(q, rd, wr)
        sem = COUNTER[q]
        for fn in fns:
            fn().then_inc(T.sem[sem], 1)
            val = bump(sem, 1)
        after(q, rd, wr, (sem, val, dict(clock[q])))

    def dma(parts, rd, wr, sem=None, add=False):
        if sem is None:
            sem = "d%d" % nd[0]
            nd[0] += 1
        clk = {}
        for q in sorted(set(p[0] for p in parts)):
            before(q, rd, wr)
            for s_, v_ in clock[q].items():
                clk[s_] = max(clk.get(s_, 0), v_)
        for (q, o, i) in parts:
            if sem == "gd0":
                g.dma_start(o, i, allow_slow_non_contiguous=True).then_inc(T.sem[sem], 16)
            elif add:
                g.dma_start(o, i, accum_op=AluOpType.add).then_inc(T.sem[sem], 16)
            else:
                eng[q].dma_start(o, i).then_inc(T.sem[sem], 16)
            val = bump(sem, 16)
        after("dma", rd, wr, (sem, val, clk))

    def exchange(kind, src, t, only):
        name, win, land, plan = kinds_of(t)[kind]
        dst, asem, lsem = "%s%d" % (win, t % 2), "a%s%d" % (name, t), "l%s%d" % (name, t)
        calls = calls_of(core, cores, topo, plan)
        for cl in (calls[int(only):int(only) + 1] if only else calls):
            before("g", [(src, (b[0][0] - 1) * S, (b[0][0] - 1 + len(b)) * S) for b, _, _ in cl], [])
            val = bump(lsem, send(g, T, topo, cl, lambda d, n: T[src][:, (d - 1) * S:(d - 1 + n) * S],
                                  lambda d, n, c_: T[dst][:, V + (d - 1) * S:V + d * S] if c_ in cores else T[land][:, 2 * t * S:(2 * t + n) * S],
                                  asem, lsem))
        if only and int(only) < len(calls) - 1:
            return
        after("dma", [(src, 0, SH)], [], (lsem, val, dict(clock["g"])))
        acc[dst] = [e for e in acc.get(dst, []) if e[0] < V]
        acc[dst].append([V, W, (asem, bump(asem, arrivals(core, cores, topo, plan)), {}), True, "dma"])

    kinds = destinations(core, cores, topo)

    def show(w, t, hn, words):
        if w[0] == "+":
            exchange("mh".index(w[1]), ("sm", "shr")["mh".index(w[1])], t, w[2:])
            return
        lo, hi = (kinds[w[1]][0][0] - 1) * S, kinds[w[1]][-1][0] * S
        pt = ("pn%d" % "MPTN".index(w[1]), 0, hi - lo)
        parts = [("v", lo, lo + S), ("a", lo + S, hi)] if w[2] == "b" else [(w[2], lo, hi)]
        if w[0] == "g" and w[2] != "m":
            for q, l, h in parts:
                before(q, [("wrot", V, 2 * V)], [])
                gather(q, ("sm", l, h), ("wrot", 0, V), ("per", 256 + l // 16, 256 + h // 16))
                after(q, [("wrot", V, 2 * V)], [], acc["wrot"][-1][2])
        elif w[0] == "g":
            z = min(t, 1)
            gtt(("sm", lo, hi), ("ff", 0, 512), ("fl", 112 * z + lo // 16, 112 * z + hi // 16), ("mk", SH * z + lo, SH * z + hi), mul)
        elif w[0] == "k":
            gather(w[2], ("mk", lo, hi), ("tb", 0, 16), ("fl", 56 + lo // 16, 56 + hi // 16))
        elif w[0] == "G":
            for q, l, h in parts:
                gather(q, ("sh", l, h), (hn, 0, V), ("nat", 312 + l // 16, 312 + h // 16))
            if "K%ss" % w[1] not in words:
                op("t", [("rot", 0, 128), ("sh", lo, hi)], [pt], lambda: g.tensor.matmul(c(*pt), T.rot[:, :], c("sh", lo, hi), True, True))
        elif w[2] == "s":
            dma([("s", T.shr[0:112, lo:hi], T.sh[16:128, lo:hi]), ("s", T.shr[112:128, lo:hi], T.sh[0:16, lo:hi])],
                [("sh", lo, hi)], [("shr", lo, hi)])
        elif w[2] == "a":
            op("a", [pt], [("shr", lo, hi)], lambda: g.scalar.activation(c("shr", lo, hi), c(*pt), F.Copy))
        else:
            cp(("shr", lo, hi), pt)

    def c(b, lo, hi):
        return T[b][:, lo // 16:hi // 16, :] if b in ("ab", "cm") else T[b][:, lo:hi]

    def ts(q_out, q_in, s1, s2, o0, o1=None, extra=()):
        if o1 is None:
            op("v", [q_in] + list(extra), [q_out], lambda: g.vector.tensor_scalar(c(*q_out), c(*q_in), s1, None, o0))
        else:
            op("v", [q_in] + list(extra), [q_out], lambda: g.vector.tensor_scalar(c(*q_out), c(*q_in), s1, s2, o0, o1))

    def tt(q_out, a, b, o):
        op("v", [a, b], [q_out], lambda: g.vector.tensor_tensor(c(*q_out), c(*a), c(*b), o))

    def cp(q_out, q_in):
        op("v", [q_in], [q_out], lambda: g.vector.tensor_copy(c(*q_out), c(*q_in)))

    def gather(q, out, win, off):
        if q == "v":
            op("v", [win, off], [out], lambda: g.vector.tensor_copy(c(*out), c(*win).indirect(c(*off))))
        else:
            op("a", [win, off], [out], lambda: g.scalar.activation(c(*out), c(*win).indirect(c(*off)), F.Copy))

    def gtt(out, win, off, b, o):
        op("v", [win, off, b], [out], lambda: g.vector.tensor_tensor(c(*out), c(*win).indirect(c(*off)), c(*b), o))

    def fold(j):
        for bank in ("pa0", "pa1")[:2 - 2 * j]:
            op("t", [("zer", 0, 512)], [(bank, 0, 256)],
               lambda: g.tensor.matmul(c(bank, 0, 256), c("zer", 0, 128), c("zer", 0, 256), True, False))
        for z in range(2):
            bank = "pa%d" % z
            op("t", [("fw", 0, 576), ("xx", 256 * j, 256 * j + 256)], [(bank, 0, 256)],
               *[lambda b=b, r=r: g.tensor.matmul(c(bank, 128 * (b % 2), 128 * (b % 2) + 128), c("fw", 144 * b + 3 - r, 144 * b + 131 - r),
                                                  T.xx[:, r, :], False, b % 2 == 1 and r == 3)
                 for b in (2 * z, 2 * z + 1) for r in (2 * j, 2 * j + 1)])

    def copy(q, out, in_):
        if q == "v":
            cp(out, in_)
        else:
            act(out, in_, F.Copy)

    def moved(j):
        dma([("s", T.wrot[r:128:16, :], T.xx[:, r, :]) for r in (2 * j, 2 * j + 1)],
            [("xx", 256 * j, 256 * j + 256)], [("wrot", V * j, V * j + V)])

    def unlist(wm):
        dma([("s", T[wm][16 + r:128:16, 0:V], T.xx[0:112, r, :]) for r in range(4)]
            + [("s", T[wm][r:r + 1, 0:V], T.xx[112:128, r, :]) for r in range(4)], [("xx", 0, 512)], [(wm, 0, V)])

    def high(q, src, lo, hi, j=0):
        o = T.xx[:, 2 * j:2 * j + 2, lo:hi]
        op(q, [src], [("xx", 256 * j + 2 * lo, 256 * j + 2 * hi)],
           lambda: g.vector.tensor_copy(o, c(*src)) if q == "v" else g.scalar.activation(o, c(*src), F.Copy))

    def low(src, lo, hi):
        op("v", [src, ("xx", 2 * lo, 2 * hi)], [("xx", 256 + 2 * lo, 256 + 2 * hi)],
           lambda: g.vector.tensor_tensor(T.xx[:, 2:4, lo:hi], c(*src), T.xx[:, 0:2, lo:hi], sub))

    LC = [0, 128, 64, 192]
    PA = [("pa0", 0, 64), ("pa1", 0, 64), ("pa0", 64, 128), ("pa1", 64, 128)]

    def act(out, in_, func, **kw):
        op("a", [in_], [out], lambda: g.scalar.activation(c(*out), c(*in_), func, **kw))

    eq = AluOpType.is_equal
    sn_ = ("li", 256, 312)

    def col(j):
        return c("pc", j, j + 1)

    def diagonal(name, f, down=0):
        o, z = (name, 0, 128), ({"float32": "zf", "bfloat16": "zer", "float16": "z2"}[SCRATCH[name][2]], 0, 128)
        for base in ((-down, 128 - down) if down else (0,)):
            op("g", [z], [o], lambda: g.affine_select(c(*o), c(*z), [[-1, 128]], AluOpType.not_equal, f, base, 1))
            z = o

    dma([("s", T.mi[0:112, 0:128], T.mm[1:8, :]), ("a", T.mi[0:112, 128:256], T.mt[1:8, :]),
         ("s", T.mi[112:128, 0:128], T.mm[0:1, :]), ("a", T.mi[112:128, 128:256], T.mt[0:1, :])], [], [("mi", 0, 256)])
    dma([("s", T.li[0:112, 256:312], T.sn[16:128, :]), ("a", T.li[112:128, 256:312], T.sn[0:16, :])], [], [sn_])
    dma([("a", c("li", 312, 368), T.sn[:])], [], [("li", 312, 368)])
    dma([("s", c("hw0", 0, H0), T.h0[:, 0:H0])], [], [("hw0", 0, H0)])
    op("g", [], [("pi", 0, 1)], lambda: g.iota(c("pi", 0, 1), [[0, 1]], 0, 1))
    op("g", [], [("jr", 0, 144)], lambda: g.iota(c("jr", 0, 144), [[1, 144]], -15, 0, allow_small_or_imprecise_dtypes=True))
    op("g", [], [("jq", 0, 16)], lambda: g.iota(c("jq", 0, 16), [[1, 4], [0, 4]], 0, 0, allow_small_or_imprecise_dtypes=True))
    for b, n in (("zer", 512), ("fw", 576), ("zf", 128)):
        op("v", [], [(b, 0, n)], lambda: g.vector.memset(c(b, 0, n), 0.0))
    for j in range(4):
        act(("wm0", 512 * j, 512 * j + 512), ("zer", 0, 512), F.Copy)
    for b in range(4):
        op("g", [("zer", 0, 32)], [("fw", 144 * b, 144 * b + 144)], lambda: g.affine_select(
            T.fw[:, 144 * b + 3:144 * b + 131:4], c("zer", 0, 32), [[-4, 32]], AluOpType.not_equal, 1.0, -b, 1))
    diagonal("rot", 1.0, 16)
    op("g", [], [("vi", 0, 64)], lambda: g.iota(c("vi", 0, 64), [[16, 64]], 512, 1, allow_small_or_imprecise_dtypes=True))
    op("g", [], [("ti", 0, 32)], lambda: g.iota(c("ti", 0, 32), [[1, 32]], 0, 32))
    for name, f in (("idn", 1.0), ("hi", 0.5), ("ni", -0.5), ("hib", 0.5)):
        diagonal(name, f)
    ts(("pi", 1, 2), ("pi", 0, 1), 112, None, band)
    ts(("pi", 2, 3), ("pi", 0, 1), 1, None, band)
    ts(("pi", 3, 4), ("pi", 0, 1), 2, 3, shr_, band)
    cp(("pc", 0, 4), ("pi", 0, 4))
    ts(("tb", 0, 16), ("jq", 0, 16), col(3), None, eq, extra=[("pc", 3, 4)])
    ts(("pc", 4, 5), ("pc", 2, 3), -4.0, 4.0, mul, add)
    ts(("mi", 0, 128), ("mi", 0, 128), 1023, None, band)
    cp(("ps", 128, 256), ("mi", 128, 256))
    cp(("ps", 0, 128), ("mi", 0, 128))
    ts(("si", 56, 112), sn_, 7, None, shr_)
    high("v", ("ps", 0, 256), 0, 128)
    ts(("si", 0, 56), sn_, 511, None, band)
    fold(0)
    low(("ps", 0, 256), 0, 128)
    fold(1)
    cp(("fl", 0, 112), ("si", 0, 112))
    cp(("nat", 312, 368), ("li", 312, 368))
    ts(("em", 0, 144), ("jr", 0, 144), col(1), col(2), eq, mul, extra=[("pc", 0, 4)])
    ts(("ec", 0, 144), ("jr", 0, 144), col(1), None, eq, extra=[("pc", 0, 4)])
    for z in range(2):
        cp(("ff", 256 * z, 256 * z + 256), ("pa%d" % z, 0, 256))
    for w in FIRST.split():
        if w == "*o":
            unlist("wm0")
        elif w == "*h":
            dma([("s", c("hw0", H0, V), T.h0[:, H0:V])], [], [("hw0", H0, V)])
        elif w == "*p":
            dma([("s", c("li", 0, 256), T.pd[:]), ("s", c("lbi", 0, 256), T.lb[:]), ("s", c("ob", 0, 4), T.obs[:])], [],
                [("li", 0, 256), ("lbi", 0, 256), ("ob", 0, 4)])
        elif w == "*t":
            dma([("s", c("tw", 0, WV), T.wv[:, 0:WV])], [], [("tw", 0, WV)])
        elif w == "*w":
            dma([("s", c("tw", WV, A), T.wv[:, WV:A])], [], [("tw", WV, A)])
        else:
            show(w, 0, "hw0", FIRST.split())
    cp(("pa1", 0, 256), ("lbi", 0, 256))
    ts(("ex", 0, 144), ("jr", 0, 144), col(1), col(4), eq, mul, extra=[("pc", 0, 5)])
    cp(("z2", 0, 128), ("zer", 0, 128))
    for j, keep in enumerate((1024, A)):
        op("v", [], [("cb", 64 * j, 64 * j + 64)], lambda: g.vector.memset(c("cb", 64 * j, 64 * j + 64), 192.0 * keep))
    cp(("nat", 0, 256), ("li", 0, 256))
    act(("lbh", 0, 256), ("pa1", 0, 256), F.Copy)
    act(("tw", A, A + WV), ("tw", 0, WV), F.Copy)
    dma([("g", c("tc", 0, 1), T.th[:])], [], [("tc", 0, 4)], sem="gd0")
    for name, f in (("hi2", 0.5), ("ni2", -0.5), ("i512", 512.0)):
        diagonal(name, f)
    for name, f in (("hr2", 0.5), ("hr", 0.5), ("nr", -0.5), ("or2", 1.0)):
        diagonal(name, f, 16)
    diagonal("oi", 1.0)
    for b, n in (("wrot", 2 * V), ("wm1", V)):
        op("g", [], [(b, 0, n)], lambda: g.iota(c(b, 0, V), [[0, V]], 0, 0, allow_small_or_imprecise_dtypes=True))
    op("g", [], [("r1", 0, 512)], lambda: g.iota(c("r1", 0, 512), [[0, 512]], 0, 0, allow_small_or_imprecise_dtypes=True))
    act(("y8", 0, 4), ("ob", 0, 4), F.Copy, scale=0.125)
    ts(("t2", 0, 312), ("li", 0, 312), 4, None, shr_)
    ts(("f1", 0, 312), ("li", 0, 312), 2047.0, 127.0, AluOpType.min, mul)
    ts(("ps", 0, 312), ("t2", 0, 312), 127.0, -2047.0, AluOpType.min, mul)
    for h in range(2):
        ts(("pa2", 128 * h, 128 * h + 64), ("vi", 0, 64), col(1), 2.0, sub, mul, extra=[("pc", 1, 2)])
        tt(("pa2", 128 * h + 64, 128 * h + 128), ("li", 64 * h, 64 * h + 64), ("li", 128 + 64 * h, 192 + 64 * h), add)
    act(("kh", 0, 256), ("pa2", 0, 256), F.Copy)
    act(("tw", A + WV, 2 * A - WC), ("tw", WV, A - WC), F.Copy)
    cp(("tw", 2 * A - WC, 2 * A), ("tw", A - WC, A))
    tt(("ps", 0, 312), ("ps", 0, 312), ("f1", 0, 312), add)
    tt(("lbl", 0, 256), ("pa1", 0, 256), ("lbh", 0, 256), sub)
    tt(("ps", 0, 312), ("ps", 0, 312), ("li", 0, 312), add)
    ts(("ti", 0, 32), ("ti", 0, 32), 511, None, band)
    cp(("per", 0, 312), ("ps", 0, 312))
    cp(("tl", 0, 32), ("ti", 0, 32))
    tt(("ps", 384, 512), ("li", 128, 256), ("li", 0, 128), sub)
    tt(("kl", 0, 256), ("pa2", 0, 256), ("kh", 0, 256), sub)
    op("v", [("zer", 0, 128)], [("x2", 1, 2), ("x2", 5, 6)], lambda: g.vector.tensor_copy(T.x2[:, 1:8:4, :], c("zer", 0, 128)))

    def listmm(out, wt, src, slo, start, stop, pre=(), rows=range(16), book=None):
        fns = list(pre)
        for i in rows:
            x = T.cm[:, slo // 16:slo // 16 + 64, i] if src == "cm" else T[src][:, slo + i:slo + 1024:16]
            fns.append(lambda i=i, x=x: g.tensor.matmul(c(*out), T[wt][:, 15 - i:143 - i], x, start and i == 0, stop and i == 15))
        rd = [(wt, 0, 144), book or (src, slo, slo + 1024)]
        if pre:
            rd += [("idn", 0, 128), ("lbh", 0, 256), ("lbl", 0, 256), ("cb", 0, 128)]
        op("t", rd, [out], *fns)

    def xq(j, n=1):
        return ("xq", j, j + n)

    def xt(b, h):
        return ("xt", 128 * b + 64 * h, 128 * b + 64 * h + 64)

    def mm(items):
        op("t", [(i[1], 0, 128) for i in items] + [i[2] for i in items], [i[0] for i in items],
           *[lambda i=i: g.tensor.matmul(c(*i[0]), T[i[1]][:, :], c(*i[2]), i[3], i[4]) for i in items])

    def turn(q):
        before(q, [("r1", 512, 514)], [])
        gather(q, ("r2", 0, 512), ("r1", 0, 512), ("tl", 0, 32))
        dma([("a", T.ymm[:], T.r2[0:64, 0:256]), ("a", T.ymt[:], T.r2[0:64, 256:512])], [("r2", 0, 512)], [])

    for t in range(NS):
        last = t == NS - 1
        hw, hn = "hw%d" % (t % 2), "hw%d" % ((t + 1) % 2)
        wm, wn = "wm%d" % (t % 2), "wm%d" % ((t + 1) % 2)
        ml = "nat" if t == 0 else "per"
        words = (LAST if last else STEP).split()
        two, keep = ("", A) if last else ("2", 1024)
        big = 192.0 * keep
        half, nhalf, one, xb = ("hi", "ni", "oi", "xq") if last else ("hr", "nr", "or2", "x2")
        for w in words:
            x = w[0]
            if x == "g" or w == "+m":
                show(w, t + 1, hn, words)
                continue
            if x in "GK+":
                if t:
                    show(w, t, hw, words)
                continue
            if x in "euwvyz":
                a_, b_ = [int(z) for z in w[-3:].split("-")]
                h, lo, hi = a_ // 4, 256 * a_, 256 * b_ + 256
                l1 = ("lst", 128 * h + (lo - 1024 * h) // 16, 128 * h + (hi - 1024 * h) // 16)
                if x == "e":
                    o, win = ("ee", lo, hi), ("pp", 2048 * h, 2048 * h + 2048)
                    if w[1] == "a":
                        op("a", [win, l1, ("y8", 0, 4)], [o], lambda: g.scalar.activation(
                            c(*o), c(*win).indirect(c(*l1)), F.Identity, bias=c("y8", t, t + 1), scale=-0.125))
                    else:
                        op("v", [win, l1, ("y8", 0, 4)], [o], lambda: g.vector.tensor_scalar(
                            c(*o), c(*win).indirect(c(*l1)), -0.125, c("y8", t, t + 1), mul, add))
                elif x == "u":
                    gtt(("uu", lo, hi), ("wa", 2048 * h, 2048 * h + 2048), l1, ("ee", lo, hi), mul)
                elif x == "v":
                    gather(w[1], ("hp", lo, hi), (hw, 0, W), ("lst", l1[1] + 64, l1[2] + 64))
                    mm([((YB[a_ // 2], 0, hi - lo), "oi", ("hp", lo, hi), True, False)])
                elif x == "y":
                    mm([((YB[a_ // 2], 0, hi - lo), "oi", ("uu", lo, hi), False, True)])
                elif x == "z":
                    copy(w[1], (hn, lo, hi), (YB[a_ // 2], 0, hi - lo))
                    if last:
                        dma([("s", T.yh[:, lo:hi], c(hn, lo, hi))], [(hn, lo, hi)], [])
                else:
                    gtt((hn, lo, hi), (hw, 0, W), ("lst", l1[1] + 64, l1[2] + 64), ("uu", lo, hi), add)
                    if last:
                        dma([("s", T.yh[:, lo:hi], c(hn, lo, hi))], [(hn, lo, hi)], [])
                continue
            k = int(w[1])
            if x in "EZ" and w[-2:] in (".a", ".b"):
                rows, book = (range(CUT), ("cm", 1024 * k, 1024 * k + 1024)) if w[-1] == "a" else (range(CUT, 16), ("cm", A + k, A + k + 1))
                if x == "E":
                    o, i_ = (T[b][:, 64 * k:64 * k + 64, rows[0]:rows[-1] + 1] for b in ("cm", "ab"))
                    op("v", [("ab", 1024 * k, 1024 * k + 1024), ("tc", 0, 1)], [book],
                       lambda: g.vector.tensor_scalar(o, i_, c("tc", 0, 1), None, AluOpType.is_gt))
                else:
                    listmm(("pn%d" % k, 64 - 64 * (k % 2), 128 - 64 * (k % 2)), "ec", "cm", 1024 * k, False, True, rows=rows, book=book)
                continue
            if x in "ABCDSE":
                j, n = (int(w[-1]), 512) if "." in w else (0, 1024)
                r = (1024 * k + 512 * j, 1024 * k + 512 * j + n)
                l0, l1 = 32 * j, 32 * j + n // 16
            p0, p1, sg = "pn%d" % (2 * k), "pn%d" % (2 * k + 1), ("sg", 64 * k, 64 * k + 64)
            pn = ("pn%d" % k, 64 - 64 * (k % 2), 128 - 64 * (k % 2))
            if x == "A":
                gather(w[2], ("mp",) + r, (wm, 0, W), (ml, LC[k] + l0, LC[k] + l1))
            elif x == "X":
                listmm(PA[k], "ex", "mp", 1024 * k, False, True, pre=[
                    lambda: g.tensor.matmul(c(*PA[k]), T.idn[:, :], c("lbh", LC[k], LC[k] + 64), True, False),
                    lambda: g.tensor.matmul(c(*PA[k]), T.idn[:, :], c("lbl", LC[k], LC[k] + 64), False, False),
                    lambda: g.tensor.matmul(c(*PA[k]), T.idn[:, :], c("cb", 64 * last, 64 * last + 64), False, False)])
            elif x == "Y":
                listmm(pn, "em", "mp", 1024 * k, True, False)
            elif x == "Z":
                listmm(pn, "ec", "cm", 1024 * k, False, k % 2 == 0 or words.index("N%d" % (k // 2)) < words.index(w))
            elif x == "o":
                ts(("al", 64 * k, 64 * k + 64), PA[k], -big, None, add)
            elif x == "i":
                op("v", [("pa%d" % k, 0, 128), ("xt", 128 * k, 128 * k + 128)], [(xb, j, j + 1) for j in (2 * k, 2 * k + 4)],
                   lambda: g.vector.tensor_tensor(T[xb][:, 2 * k:8:4, :], c("pa%d" % k, 0, 128), c("xt", 128 * k, 128 * k + 128), sub))
            elif x == "j":
                act(("xt", 128 * k, 128 * k + 128), ("pa%d" % k, 0, 128), F.Identity, bias=-(keep - 1) / 2)
            elif x == "B":
                gather(w[2], ("wa",) + r, ("tw", 0, 2 * A), ("al", 64 * k + l0, 64 * k + l1))
            elif x == "C":
                gtt(("pp",) + r, (hw, 0, W), ("nat", LC[k] + l0, LC[k] + l1), ("wa",) + r, mul)
            elif x == "D":
                op("a", [("pp",) + r, ("ob", 0, 4)], [("ab",) + r],
                   lambda: g.scalar.activation(c("ab", *r), c("pp", *r), F.Abs, bias=c("ob", t, t + 1), scale=-1.0))
            elif x == "S":
                if "nt" not in acc:
                    act(("nt", 0, 1), ("tc", 0, 1), F.Copy, scale=-1.0)
                op("a", [("ab",) + r, ("nt", 0, 1)], [("df",) + r],
                   lambda: g.scalar.activation(c("df", *r), c("ab", *r), F.Identity, bias=c("nt", 0, 1), scale=1.0))
            elif x == "E":
                if "S" + w[1:] in words or "S" + w[1] in words:
                    ts(("cm",) + r, ("df",) + r, 0.0, None, AluOpType.is_gt)
                else:
                    ts(("cm",) + r, ("ab",) + r, c("tc", 0, 1), None, AluOpType.is_gt, extra=[("tc", 0, 1)])
            elif x == "x":
                for h in range(2):
                    o = ("pa2", 128 + 64 * h, 192 + 64 * h)
                    mm([(o, "hi" + two, (xb, 4 * h + 2, 4 * h + 3), True, False), (o, "ni" + two, (xb, 4 * h, 4 * h + 1), False, True)])
            elif x == "n":
                act(xq(4 * k + 1), (p0, 64, 128), F.Identity, scale=2.0)
            elif x == "N":
                mm([((p1, 0, 64), "ni", xq(4 * k + 1), False, "Z%d" % (2 * k + 1) in words[:words.index(w)])])
            elif x == "Q":
                mm([((p0, 0, 128), half + two, (xb, 4 * k, 4 * k + 2), True, False),
                    ((p0, 0, 64), half + two, (xb, 4 * k + 2, 4 * k + 3), False, False)]
                   + ([] if last else [((p0, 64, 128), half, xq(4 * k + 1), False, False)]))
            elif x == "s":
                act(sg, (p1, 0, 64), F.Sign, scale=-1.0, bias=-0.5)
            elif x == "M":
                act(("rr",) + sg[1:], (p1, 0, 64), F.Relu, scale=-2.0)
            elif x == "r":
                mm([((p0, 64, 128), nhalf, ("rr",) + sg[1:], False, words.index("m%d" % k) < words.index(w))])
            elif x == "t":
                tt(("tm" + two,) + sg[1:], ("pa2", 128 + 64 * k, 192 + 64 * k), sg, mul)
            elif x == "m":
                mm([((p0, 0, 64), one, ("tm" + two,) + sg[1:], False, words.index("r%d" % k) < words.index(w))])
            elif x == "h":
                if last:
                    for j in range(2):
                        op("a", [(p0, 0, 128)], [("qq", 2 * k + j, 2 * k + j + 1)], lambda: g.scalar.activation(
                            T.qq[:, 8 * k + j:8 * k + 8:2, :], c(p0, 64 * j, 64 * j + 64), F.Copy))
                else:
                    high(w[2], (p0, 0, 128), 64 * k, 64 * k + 64)
            elif x == "l":
                low((p0, 0, 128), 64 * k, 64 * k + 64)
            elif x == "U":
                if k < 2:
                    moved(k)
                else:
                    unlist(wn)
            elif x == "p":
                tt(("tp",) + sg[1:], ("ps", 384 + 64 * k, 448 + 64 * k), sg, mul)
            elif x == "q":
                mm([((p1, 64, 192), "hib", ("kh", 128 * k, 128 * k + 128), True, False),
                    ((p1, 64, 192), "hib", ("kl", 128 * k, 128 * k + 128), False, False), ((p1, 64, 128), "i512", sg, False, False),
                    ((p1, 128, 192), "hi", ("tp",) + sg[1:], False, True)])
            elif x == "c":
                cp(("lst", 128 * k, 128 * k + 128), (p1, 64, 192))
            elif x == "O":
                dma([("s", T.r1[b:64:8, :], T.qq[:, 2 * b:2 * b + 2, :]) for b in range(4 * k, 4 * k + 4)],
                    [("qq", 2 * k, 2 * k + 2), ("r1", 0, 512)], [("r1", 512 + k, 513 + k)])
            elif x == "R":
                turn("a")

    for sem in order:
        if waited.get(sem, 0) < count[sem]:
            g.wait_ge(T.sem[sem], count[sem])
